import numpy as np, ml_dtypes
CORES = [40,64,80,88,96,104,120,144]
N = 8
import mx_ref
BF = ml_dtypes.bfloat16
def gcols(t, e):
    v = np.concatenate([t.reshape(8, 16, -1, 4), np.zeros((8, 16, 1, 4), BF)], axis=2)
    return np.ascontiguousarray(np.stack([v[g][:, e[g]] for g in range(8)])).reshape(128, -1)
def tile(rs):
    return np.stack(rs, axis=2).reshape(128, -1).astype(BF)
def pick(q, e):
    c = np.concatenate([q[0].reshape(128, -1, 4), np.zeros((128, 1, 4), np.uint8)], axis=1); s = np.concatenate([q[1], np.ones((16, 1), np.uint8)], axis=1)
    return (np.ascontiguousarray(c[:, e].reshape(128, -1)), np.ascontiguousarray(s[:, e]))
def join(*qs):
    return (np.concatenate([q[0] for q in qs], axis=1), np.concatenate([q[1] for q in qs], axis=1))
def put(q, e, v):
    c, s = q[0].reshape(128, -1, 4).copy(), q[1].copy(); c[:, e] = v[0].reshape(128, -1, 4); s[:, e] = v[1]
    return (c.reshape(128, -1), s)
def pk(c, s):
    return (np.ascontiguousarray(c), mx_ref.live(s))
def emit(q):
    return q[0], q[1]
def packed(v, rng):
    q = [mx_ref.quantize(np.ascontiguousarray(v[r])) for r in range(N)]
    return np.stack([a for a, b in q]), np.stack([mx_ref.plane(b, rng) for a, b in q])
def values_of_codes():
    e, c = np.zeros((128, 128, 4), np.float32), np.zeros((128, 2, 4), np.uint8)
    e[np.arange(128), np.arange(128), 0] = 1
    c[:127, :, 0] = np.arange(256).reshape(2, 128).T[:127]
    return mx_ref.matmul(mx_ref.quantize(e.reshape(128, 512).astype(BF)), (c.reshape(128, 8), np.full((16, 2), 127, np.uint8))).T.reshape(-1).astype(np.float64)
CODE_VALUE, SCALE_VALUE = values_of_codes(), 2.0 ** (np.arange(256) - 127.0)
def decode(q):
    return (CODE_VALUE[q[0]].reshape(16, 8, -1, 4) * SCALE_VALUE[q[1]][:, None, :, None] + 0.0).reshape(128, -1).astype(np.float32)
def f(rng, *shape):
    return mx_ref.flush((rng.standard_normal(shape, dtype=np.float32) * np.exp2(rng.integers(-2, 3, shape[:-1] + (1,)))).astype(BF))
def wide(rng, *shape, cols=0):
    v = rng.standard_normal(shape, dtype=np.float32) * np.exp2(rng.integers(-12, 13, shape)).astype(np.float32)
    if cols: v *= np.repeat(np.exp2(rng.integers(-cols, cols + 1, shape[:-2] + (1, shape[-1] // 4))) * (rng.random(shape[:-2] + (1, shape[-1] // 4)) > 0.0625), 4, axis=-1).astype(np.float32)
    return mx_ref.flush(v.astype(BF))
C, K = 320, 160
STEP = [1, 2, 4]
def numbers_of(rng):
    return {"x": np.array(f(rng, N, 128, 4 * C)), "u": np.array(f(rng, N, 128, 512)), "v": np.array(f(rng, N, 128, 512))}
def same(rng, w):
    c, s = packed(np.stack([w] * N), rng)
    return {"wc": c, "ws": np.stack([s[0]] * N)}
def weights(rng, still=[]):
    w = np.array(f(rng, 128, 2048)).reshape(8, 16, 4, 8, 16, 4)
    for i in still:
        w[:, i] = 0
        w[:, :, :, :, i] = 0
    return same(rng, w.reshape(128, 2048))
def setup_inputs(rng):
    return {**numbers_of(rng), **weights(rng)}
def setup_inputs_ties(rng):
    d = numbers_of(rng)
    x = d["x"].reshape(N, 8, 16, C, 4)
    x[:, :, 0] = 0
    x[:, :, 0, :, 0] = rng.integers(0, 3, (N, 8, C)).astype(np.float32).astype(BF)
    u = d["u"].reshape(N, 128, 128, 4)
    u[:, :, ::16] = 0
    o = rng.permutation(N)
    for r in range(N):
        for h in range(0, 128, 16): u[r, h, h, 0] = 0.0 if r == o[0] else -1.0 if r == o[1] else 1.0
    return {"x": x.reshape(N, 128, 4 * C), "u": u.reshape(N, 128, 512), "v": d["v"], **weights(rng, [0])}
def setup_inputs_near(rng):
    d = numbers_of(rng)
    x = d["x"].astype(np.float32).reshape(N, 8, 16, C, 4)
    x[:, :, 0] = 0
    x[:, :, 8:] = 0
    s = rng.integers(0, 16, (N, 8, C))
    c = rng.permuted(np.tile(np.arange(8) % 2 * 2.0 - 1.0, (N, 1)), axis=1)
    u = d["u"].reshape(N, 128, 128, 4)
    u[:, :, ::16] = 0
    o = rng.permutation(N) % 4
    for r in range(N):
        k = 1.0 if o[r] == 0 else 2.0 ** -30
        if o[r] < 2:
            x[r, :, 0, :, 0] = c[r][:, None]
            x[r, :, 11, :, 0] = 2.0 ** -10
        else:
            for g in rng.permutation(8)[:4]:
                far = int(rng.integers(C))
                x[r, g, :8, far] = 0
                x[r, g, 0, far, 0] = 2.0 ** 30 * rng.choice([-1.0, 1.0])
        if o[r] == 2:
            t = rng.integers(0, 2, (8, C)) == 1
            x[r, :, 9, :, 0] = np.where(t, 1.125 * 2.0 ** -30 * c[r][:, None], 0.0)
            x[r, :, 10, :, 0] = np.where(t, 0.0, 2.0 ** -30 * c[r][:, None])
        else: x[r, :, 8] = ((s[r][:, :, None] >> np.arange(4)) & 1) * np.exp2(np.arange(4) - 23.0)
        for h in range(0, 128, 16):
            u[r, h, h, 0] = k
            if o[r] == 2:
                u[r, h + 9, h, 0] = k * 1.125
                u[r, h + 10, h, 0] = k * 1.25
            else: u[r, h + 8, h] = k
            if o[r] < 2: u[r, h + 11, h, 0] = k
    return {"x": x.reshape(N, 128, 4 * C).astype(BF), "u": u.reshape(N, 128, 512), "v": d["v"], **weights(rng, [0, 8, 9, 10, 11, 12, 13, 14, 15])}
def setup_inputs_huge(rng):
    d = numbers_of(rng)
    o = rng.permutation(N)
    c = rng.integers(0, 2, (N, 1, 1, C, 1)) * 2.0 - 1.0
    c[o < N // 2] = -1.0
    x = (0.6 + 0.09 * rng.random((N, 8, 16, C, 4))) * c
    x[o == 0] = -0.9 - 0.1 * rng.random((1, 8, 16, C, 4))
    a = 1.0 - 0.1 * rng.random((N, 8, 16, 8, 4))
    for r in range(N): a[r] *= (rng.permutation(8) % 2 * 2.0 - 1.0)[None, None, :, None]
    u = d["u"].reshape(N, 128, 128, 4)
    u[:, :, ::16] = (2.0 ** 30 * a).reshape(N, 128, 8, 4).astype(np.float32).astype(BF)
    w = np.zeros((128, 4, 128, 4), np.float32)
    i = np.arange(128)
    for b in range(4): w[i, b, i, b] = 4
    return {"x": (2.0 ** 30 * x).astype(np.float32).reshape(N, 128, 4 * C).astype(BF), "u": u.reshape(N, 128, 512), "v": d["v"], **same(rng, w.reshape(128, 2048).astype(BF))}
def setup_inputs_jam(rng):
    d = numbers_of(rng)
    x = d["x"].reshape(N, 8, 16, C, 4)
    o = rng.permutation(N) % 4
    a = np.argsort(rng.random((N, 8, C)), axis=2) < K
    i = np.arange(C)
    for r in range(N):
        if o[r] == 0:
            a[r, ::2] = i >= C - K
            a[r, 1::2] = i < K
        if o[r] == 1: a[r] = a[r, 0].copy()
        if o[r] == 2:
            for g in range(8): a[r, g] = (i + int(rng.integers(C))) % C < K
    x[:, :, :2] = 0
    x[:, :, 0, :, 0] = np.where(a, -4.0, -3.0).astype(np.float32).astype(BF)
    x[:, :, 1, :, 0] = 1.0
    t = (1.0 + (2 * rng.integers(0, 64, (N, 8, 8, C, 4)) + 1) / 128.0) * np.exp2(rng.integers(-14, -8, (N, 8, 8, C, 4))) * (rng.integers(0, 2, (N, 8, 8, C, 4)) * 2.0 - 1.0)
    x[:, :, 8:] = t.astype(np.float32).astype(BF)
    x[:, :, 8, :, 0] = 1.96875
    u = d["u"].reshape(N, 128, 128, 4)
    u[:, :, ::16] = 0
    for h in range(0, 128, 16): u[:, h, h, 0] = -1.0
    for r in range(N):
        if o[r] == 3:
            x[r, :, 0, :, 0] = -4.0
            x[r, :, 9] = 0
            x[r, :, 9, :, 0] = (np.where(a[r], 4.0, 3.0) * np.exp2(-13.0 - np.arange(8) % 4)[:, None]).astype(np.float32).astype(BF)
            for h in range(0, 128, 16): u[r, h + 9, h, 0] = 1.0
    w = np.array(f(rng, 128, 2048)).reshape(8, 16, 4, 8, 16, 4)
    w[:, :, :, :, :2] = 0
    w[:, :, :, :, 8:] = 0
    return {"x": x.reshape(N, 128, 4 * C), "u": u.reshape(N, 128, 512), "v": d["v"], **same(rng, fall(w))}
def fall(v):
    for g in range(8): v[g, 1, 0, g, 0, 0] = 128.0
    return v.reshape(128, 2048)
def setup_inputs_spread(rng):
    d = setup_inputs(rng)
    d["x"] = wide(rng, N, 128, 4 * C, cols=6)
    return d
def check_inputs(d):
    b = []
    for k in ("x", "u", "v"):
        a = np.abs(d[k].astype(np.float32))
        if not (np.isfinite(a).all() and ((a == 0) | (a >= 2.0 ** -30) & (a <= 2.0 ** 30)).all()): b.append("a value of " + k)
    if ((d["wc"] & 0x7F) == 0x7F).any(): b.append("a code of wc that is no number")
    for k in ("wc", "ws"):
        if (d[k] != d[k][:1]).any(): b.append(k + " isn't the same on all ranks")
    none, least, most = [emit(mx_ref.quantize(np.full((128, 16), k, np.float32).astype(BF)))[1][0, 0] for k in (0.0, 2.0 ** -30, 2.0 ** 30)]
    for r in range(N):
        s = mx_ref.live(d["ws"][r])
        if ((s != none) & ((s < least) | (s > most))).any(): b.append("a scale of ws")
    return b
def places(s):
    a = np.sort(np.argsort(-s, axis=2, kind="stable")[:, :, :K], axis=2)
    j = np.arange(K)
    c = a.copy()
    at = np.stack([j] * N)
    for g in range(7):
        n = np.sum(a[:, g + 1][:, None, :] < a[:, g][:, :, None], axis=2)
        p = np.maximum.accumulate(n - j, axis=1) + j
        for r in range(N):
            m = int(np.sum(p[r] < K))
            p[r, m:] = np.setdiff1d(j, p[r, :m])
            at[r] = p[r][at[r]]
            c[r, g + 1] = a[r, g + 1][at[r]]
    return c
def reference(x, u, v, wc, ws):
    qu = [mx_ref.quantize(u[r]) for r in range(N)]
    lay = [pk(wc[r], ws[r]) for r in range(N)]
    now = [x[r] for r in range(N)]
    for e in STEP:
        q = [mx_ref.quantize(now[r]) for r in range(N)]
        own = [decode(q[r]) for r in range(N)]
        c = places(np.stack([mx_ref.matmul(qu[r], q[r])[::16] for r in range(N)]) + np.float32(0.0))
        made = []
        for r in range(N):
            z = mx_ref.quantize(gcols(own[r].astype(BF), c[r]))
            h = tile([np.maximum(mx_ref.matmul(pick(lay[r], np.arange(128 * b, 128 * b + 128)), z), np.float32(0.0)) * np.float32(0.015625) for b in range(4)])
            made.append(decode(mx_ref.quantize(h)))
        for r in range(N):
            a, b = own[r].reshape(8, 16, C, 4).copy(), made[r ^ e].reshape(8, 16, K, 4)
            for g in range(8): a[g][:, c[r, g]] += b[g]
            now[r] = a.reshape(128, 4 * C).astype(BF)
    y, pl = np.zeros((N, 128, C), np.float32), np.zeros((N, 8, K), np.float32)
    oc, osc = np.zeros((N, 128, 4 * C), np.uint8), np.zeros((N, 16, C), np.uint8)
    for r in range(N):
        q = mx_ref.quantize(now[r])
        y[r] = mx_ref.matmul(mx_ref.quantize(v[r]), q)
        pl[r] = c[r]
        oc[r], osc[r] = emit(q)
    return {"y": y, "pl": pl, "oc": oc, "osc": osc}

@@ -1,0 +1,494 @@
+from concourse.bass import DstId, RemoteDMATransfer
+from concourse.mybir import dt, AluOpType, AxisListType, ActivationFunctionType
+
+C, K, ROUNDS = 320, 160, 3
+STEP = [1, 2, 4]
+X4, U8, U16, BF, F32, I32 = "float8_e4m3fn_x4", "uint8", "uint16", "bfloat16", "float32", "int32"
+SIZES = {
+    BF: {"xin": 4 * C, "uin": 512, "vin": 512, "brow": 256, "e0": 520, "ct": 1536, "na": C, "idr": K,
+         "cmp": 20 * C, "st": 4 * C, "eqs": C, "ne": C, "pre": C, "yy": C, "wv": C,
+         "nb": C, "pj": 400, "tb": 1376, "rw": 640, "pr": 192, "tp": 384,
+         "ca": K, "cb": K, "la": K, "lr": 192, "tl": 352, "cr": 192, "tc": 352,
+         "fw": 4 * 480, "z": 4 * K, "h": 4 * K, "xn": 4 * C},
+    F32: {"cf": 32, "small": 128, "lbt": 16, "dw": 32, "thr": K, "ts": C, "big": C, "kap": 16, "col": 8,
+          "na1": 64, "nb1": 64, "nx": 64, "ny": 96, "ur": 352, "tu": 672, "plb": K, "yb": C},
+    I32: {"ci": 8, "lui": 16},
+    U16: {"lu": 16, "lj": 4, "lc": 2, "lk": 2, "lb": 10, "osc1": 32, "ob": 144, "oll": 16, "ocl": 16, "ou": 32},
+    X4: {"qx": C, "qu": 128, "qu2": 256, "qv": 128, "qw": 512, "cq": 896, "cmq": 5 * C, "stq": C, "qz": K},
+    U8: {"sx": C, "su": 128, "su2": 256, "sv": 128, "sw": 512, "cs": 896, "cms": 5 * C, "sts": C, "sz": K},
+}
+SCRATCH = {n: ("sbuf", [128, w], d) for d in SIZES for n, w in SIZES[d].items()}
+for _r in range(ROUNDS):
+    for _n in ("out", "hop", "land"):
+        SCRATCH["%sq%d" % (_n, _r)] = ("sbuf", [128, K], X4)
+        SCRATCH["%ss%d" % (_n, _r)] = ("sbuf", [128, K], U8)
+for _b in range(8):
+    SCRATCH["ps%d" % _b] = ("psum", [128, 512], F32)
+
+POOL = {"v": 40, "s": 34, "t": 18, "g": 36, "d": 14}
+SEMAPHORES = ["%s_%d" % (q, i) for q in POOL for i in range(POOL[q])]
+SEMAPHORES += ["hop%d" % r for r in range(ROUNDS)] + ["arr%d" % r for r in range(ROUNDS)] + ["sent"]
+
+A = AluOpType
+ACT = ActivationFunctionType
+S_EXTRA = (0, 4, 6)
+
+
+def popcount(m):
+    return bin(m).count("1")
+
+
+def pieces_of(src, dst, topo):
+    c = [k for k in topo.cores_of(src) if k != src and topo.may_write(k, dst)]
+    near = [k for k in c if topo.die(k) == topo.die(src)]
+    far = [k for k in c if topo.die(k) != topo.die(src)]
+    e = topo.engines(src, near[0])
+    half = len(e) // 2
+    lo, hi = sum(1 << k for k in e[:half]), sum(1 << k for k in e[half:])
+    return [(near[0], "q", 0, K // 2, lo, 0), (far[0], "q", K // 2, K, hi, 0), (near[1], "s", 0, K, lo | hi, 1)]
+
+
+def side(T, name, r, piece):
+    v = T["%s%s%d" % (name, piece[1], r)][:, piece[2]:piece[3]]
+    return v.bitcast(dt.uint8) if piece[1] == "q" else v
+
+
+def relay_program(g, core, T, topo):
+    sent = 0
+    for r in range(ROUNDS):
+        for i, src in enumerate(T.cores):
+            if core not in topo.cores_of(src):
+                continue
+            dst = T.cores[i ^ STEP[r]]
+            mine = [p for p in pieces_of(src, dst, topo) if p[0] == core]
+            if not mine:
+                continue
+            g.wait_ge(T.sem["hop%d" % r], sum(popcount(p[4]) for p in mine))
+            rid, pid = topo.addr(dst, core)
+            for p in mine:
+                m = topo.mask(core, dst)
+                g.remote_dma(side(T, "land", r, p), side(T, "hop", r, p), T.sem["arr%d" % r], T.sem.sent, pid, rid, m)
+                sent += popcount(m)
+    if sent:
+        g.wait_ge(T.sem.sent, sent)
+
+
+def overlap(a, b):
+    if a[0] != b[0] or a[2] <= b[1] or b[2] <= a[1] or a[5] <= b[4] or b[5] <= a[4]:
+        return False
+    return not (a[3] == b[3] and a[3] > 1 and a[1] % a[3] != b[1] % b[3])
+
+
+def emit(g, T, ops):
+    Q = {"v": g.vector, "s": g.scalar, "t": g.tensor, "y": g.sync, "g": g}
+    members = {}
+    for i, o in enumerate(ops):
+        members.setdefault(o["joint"] or i, []).append(i)
+    rep = [members[o["joint"] or i][-1] for i, o in enumerate(ops)]
+    known = {q: 0 for q in Q}
+    at = [0] * len(ops)
+    waits = [[] for _ in ops]
+    seen = {}
+    for i, o in enumerate(ops):
+        deps = set()
+        for kind in "rw":
+            for reg in o[kind]:
+                for (j, kj, rj) in seen.get(reg[0], []):
+                    if rep[j] == rep[i]:
+                        continue
+                    if reg[0].startswith("ps") and ops[j]["q"] != o["q"]:
+                        deps.add(rep[j])
+                    elif (kind == "w" or kj == "w") and overlap(reg, rj):
+                        deps.add(rep[j])
+        for kind in "rw":
+            for reg in o[kind]:
+                seen.setdefault(reg[0], []).append((i, kind, reg))
+        q = o["q"]
+        for d in sorted(deps, reverse=True):
+            assert d < i
+            if not known[q] >> d & 1:
+                waits[i].append(d)
+                known[q] |= at[d] | 1 << d
+        at[i] = known[q]
+    signalled = set(d for w in waits for d in w) | set(rep[i] for i, o in enumerate(ops) if o["must"])
+    pools = {k: [] for k in POOL}
+    slot, value = {}, {}
+    for i, o in enumerate(ops):
+        q = o["q"]
+        for d in waits[i]:
+            Q[q].wait_ge(T.sem[slot[d][0]], value[d])
+            slot[d][3] = max(slot[d][3], value[d])
+        for (sem, val) in o["ext"]:
+            Q[q].wait_ge(sem, val)
+        ins = o["fn"]()
+        if rep[i] in signalled:
+            if rep[i] not in slot:
+                kind = "d" if o["dma"] else q
+                free = [] if o["dma"] else [s for s in pools[kind] if at[i] >> s[2] & 1]
+                if free:
+                    s = free[0]
+                else:
+                    s = ["%s_%d" % (kind, len(pools[kind])), 0, 0, 0]
+                    pools[kind].append(s)
+                s[2] = rep[i]
+                slot[rep[i]] = s
+            s = slot[rep[i]]
+            inc = 16 if o["dma"] else 1
+            ins.then_inc(T.sem[s[0]], inc)
+            s[1] += inc
+            value[rep[i]] = s[1]
+    for k in pools:
+        for s in pools[k]:
+            if s[1] > s[3]:
+                g.wait_ge(T.sem[s[0]], s[1])
+
+
+def rank_program(g, core, T, topo):
+    rank = T.rank_of(core)
+    if rank is None:
+        relay_program(g, core, T, topo)
+        return
+    ops = []
+
+    def V(name, lo=0, hi=None, step=1, quad=None):
+        hi = T[name].shape[1] if hi is None else hi
+        p0, p1 = (0, 128) if quad is None else (32 * quad, 32 * quad + 32)
+        cols = slice(lo, hi) if step == 1 else slice(lo, hi, step)
+        ap = T[name][:, cols] if quad is None else T[name][p0:p1, cols]
+        return (ap, [(name, lo, hi, step, p0, p1)])
+
+    def ind(win, off):
+        return (win[0].indirect(off[0]), win[1] + off[1])
+
+    def val(s):
+        return s[0] if isinstance(s, tuple) else s
+
+    def regs(*xs):
+        return [r for x in xs if isinstance(x, tuple) for r in x[1]]
+
+    def op(q, fn, r, w, joint=None, dma=False, must=False, ext=()):
+        ops.append({"q": q, "fn": fn, "r": r, "w": w, "joint": joint, "dma": dma, "must": must, "ext": ext})
+
+    def ts(out, in0, s1, o0, s2=None, o1=None):
+        if o1 is None:
+            op("v", lambda: g.vector.tensor_scalar(out[0], in0[0], val(s1), None, o0), regs(in0, s1), out[1])
+        else:
+            op("v", lambda: g.vector.tensor_scalar(out[0], in0[0], val(s1), val(s2), o0, o1), regs(in0, s1, s2), out[1])
+
+    def tt(out, a, b, o):
+        op("v", lambda: g.vector.tensor_tensor(out[0], a[0], b[0], o), regs(a, b), out[1])
+
+    def cp(out, a):
+        op("v", lambda: g.vector.tensor_copy(out[0], a[0]), regs(a), out[1])
+
+    def scatter(win, off, a):
+        op("v", lambda: g.vector.tensor_copy(win[0].indirect(off[0]), a[0]), regs(a, off), win[1])
+
+    def ms(out, c):
+        op("v", lambda: g.vector.memset(out[0], c), [], out[1])
+
+    def tr(out, a):
+        op("v", lambda: g.vector.transpose(out[0], a[0]), a[1], out[1])
+
+    def tr2(out, o0, row, r0, n, more=0):
+        tr(V(out, o0, o0 + n), V(row, r0, r0 + n))
+        tr(V(out, o0 + n, o0 + 2 * n + 32 + more), V(row, r0 - 16, r0 + n + 16 + more))
+
+    def scan(out, d0, d1, init, o0, o1):
+        op("v", lambda: g.vector.tensor_tensor_scan(out[0], d0[0], d1[0], val(init), o0, o1), regs(d0, d1, init), out[1])
+
+    def quant(q, s, a, c0=0, n=None):
+        q, s = V(q, c0, None if n is None else c0 + n), V(s, c0, None if n is None else c0 + n)
+        op("v", lambda: g.vector.quantize_mx(q[0], s[0], a[0]), regs(a), q[1] + s[1])
+
+    def act(out, a, f=ACT.Copy, bias=None, scale=None, acc=None):
+        kw = {}
+        if bias is not None:
+            kw["bias"] = val(bias)
+        if scale is not None:
+            kw["scale"] = val(scale)
+        if acc is not None:
+            kw["accum_out"] = acc[0]
+        op("s", lambda: g.scalar.activation(out[0], a[0], f, **kw), regs(a, bias, scale), regs(out, acc))
+
+    def lin(out, a, scale, bias):
+        act(out, a, ACT.Identity, bias=bias, scale=scale)
+
+    def mm(bank, n, lq, ls, l0, rq, rs, r0, start=True, stop=True, joint=None, ext=()):
+        o, a, b, c, d = V("ps%d" % bank, 0, n), V(lq, l0, l0 + 128), V(ls, l0, l0 + 128), V(rq, r0, r0 + n), V(rs, r0, r0 + n)
+        op("t", lambda: g.tensor.matmul_mx(o[0], a[0], b[0], c[0], d[0], start, stop), regs(a, b, c, d), o[1], joint=joint, ext=ext)
+
+    def iota(out, pat, base, cm=0, whole=False):
+        if whole:
+            op("g", lambda: g.iota(out[0], pat, base, cm), [], out[1])
+        else:
+            op("g", lambda: g.iota(out[0], pat, base, cm, allow_small_or_imprecise_dtypes=True), [], out[1])
+
+    def fill(name, lo, hi, c, step=1):
+        iota(V(name, lo, hi, step), [[0, len(range(lo, hi, step))]], c)
+
+    def mark(out, pat, base, c):
+        op("g", lambda: g.affine_select(out[0], out[0], pat, A.not_equal, c, base, 1), out[1], out[1])
+
+    def dma(q, out, a, r, w, must=False):
+        e = g.sync if q == "y" else g.scalar
+        op(q, lambda: e.dma_start(out, a), r, w, dma=True, must=must)
+
+    def P(b, n=C):
+        return V("ps%d" % b, 0, n)
+
+    def cf(k):
+        return V("cf", k, k + 1)
+
+    def ci(k):
+        return V("ci", k, k + 1)
+
+    dma("s", T.uin[:], T.u[:], [], V("uin")[1])
+    dma("y", T.xin[:], T.x[:], [], V("xin")[1])
+    dma("y", T.qw[:].bitcast(dt.uint8), T.wc[:], [], V("qw")[1])
+    dma("y", T.sw[:], T.ws[:], [], V("sw")[1])
+    dma("y", T.vin[:], T.v[:], [], V("vin")[1])
+
+    ms(V("e0"), 0.0)
+    ms(V("ct", 0, 512), 0.0)
+    iota(ci(0), [[0, 1]], 0, 1, whole=True)
+    iota(V("lui"), [[16, 2], [32, 4], [0, 2]], 0, whole=True)
+    mark(V("e0", 4, 516, 4), [[-1, 128]], 0, 1.0)
+    iota(V("brow", 0, 128), [[0, 2], [-2, 2], [0, 32]], 1)
+    op("g", lambda: g.affine_select(T.brow[:, 128:256], T.brow[:, 0:128], [[1, 2], [0, 32], [-1, 2]], A.is_equal, 0.0, 0, 0),
+       V("brow", 0, 128)[1], V("brow", 128, 256)[1])
+    fill("ct", 512, 1536, 0)
+    for t, row, w in ((0, 0, 1.0), (0, 8, -1.0), (2, 0, 1.0)):
+        mark(V("ct", 512 + t, 1024, 4), [[-16, 8], [0, 16]], -row, w)
+        mark(V("ct", 1024 + t, 1536, 4), [[-16, 8], [-1000, 2], [0, 8]], -16 - row, w)
+    fill("st", 3, 4 * C, 0, 4)
+    fill("st", 1, 4 * C, 0, 4)
+    iota(V("small", 0, 4), [[-8, 2], [256, 2]], 8)
+    iota(V("small", 8, 16), [[1, 8]], 0)
+    iota(V("small", 16, 18), [[16, 2]], 0)
+    iota(V("small", 32, 64), [[16, 32]], C)
+    iota(V("small", 64, 96), [[16, 32]], -K)
+    fill("pj", 0, 17, -K)
+    fill("pj", 337, 353, 0)
+    iota(V("idr"), [[1, K]], 0)
+    for name, n in (("pr", K), ("lr", K), ("cr", K), ("ur", C)):
+        fill(name, 0, 16, 0)
+        fill(name, 16 + n, T[name].shape[1], 0)
+    iota(V("thr"), [[1, K]], C)
+
+    ts(ci(1), ci(0), 4, A.arith_shift_right)
+    ts(ci(2), ci(0), 15, A.bitwise_and)
+    ts(ci(3), ci(0), 3, A.arith_shift_right, 1, A.bitwise_and)
+    ts(ci(4), ci(0), 4, A.arith_shift_right, 1, A.bitwise_and)
+    ts(ci(5), ci(0), 1, A.bitwise_and)
+    ts(ci(6), ci(0), 2, A.arith_shift_right, 3, A.bitwise_and)
+    cp(V("lu"), V("lui"))
+    cp(V("cf", 0, 7), V("ci", 0, 7))
+    for b in range(4):
+        quant("cq", "cs", V("e0", 4 - b, 516 - b), 128 * b, 128)
+    GRP, QQ, UP, ODD = cf(1), cf(2), cf(3), cf(4)
+    SG, TH, RB, SGS, INIT, TA, PAR, Q16, C336, C176, GO, BQ = [cf(k) for k in range(8, 20)]
+    SH = cf(23)
+    n0, n1 = 32.0 * len(S_EXTRA), 320.0
+    lin(SG, UP, -2.0, 1.0)
+    lin(cf(20), ODD, (n0 - n1) / 1024, (319.5 - n0) / 1024)
+    lin(RB, UP, 160.0 / 512, 0.0)
+    lin(SGS, UP, -2.0 / 512, 1.0 / 512)
+    lin(INIT, UP, 321.0 / 512, -161.0 / 512)
+    act(TA, cf(6), ACT.Relu, bias=-2.0)
+    lin(TH, cf(20), SG, 0.0)
+    for a in range(4):
+        lin(V("ct", 128 * a, 128 * a + 128, quad=a), V("brow", 128, 256, quad=a), 2.0 ** -10, 0.0)
+    lin(SH, TH, 1.0, 160.5 / 1024)
+
+    quant("qu", "su", V("uin"))
+    op("v", lambda: g.vector.tensor_copy(T.qu2[:, 0:256].bitcast(dt.uint32), T.qu[:, 0:128].bitcast(dt.uint32).indirect(T.lu[:, 0:16])),
+       regs(V("qu"), V("lu")), V("qu2")[1])
+    op("s", lambda: g.scalar.activation(T.su2[:, 0:256], T.su[:, 0:128].indirect(T.lu[:, 0:16]), ACT.Copy),
+       regs(V("su"), V("lu")), V("su2")[1])
+    quant("qx", "sx", V("xin"))
+
+    sent = 0
+    for r in range(ROUNDS):
+        partner = T.cores[rank ^ STEP[r]]
+        fill("rw", K, 2 * K, 200)
+        iota(V("ur", 16, 16 + C), [[1, C]], 0)
+        mm(0, 128, "qu", "su", 0, "qx", "sx", 0)
+        mm(2, C, "qu2", "su2", 0, "qx", "sx", 0)
+        mm(4, C - 128, "qu", "su", 0, "qx", "sx", 128)
+        mm(3, C, "qu2", "su2", 128, "qx", "sx", 0)
+        mm(1, C, "qu2", "su2", 0, "qx", "sx", 0)
+        tr(V("ts", 0, 128), P(0, 128))
+        tr(V("ts", 128, C), P(4, C - 128))
+        if r == 0:
+            quant("cq", "cs", V("ct", 0, 512), 512, 128)
+
+        def cmp_out(b, hh):
+            k = b // 2
+            return V("cmp", 4 * C * k + 2 * (b % 2) + hh, 4 * C * (k + 1), 4)
+
+        def s_cmp(b, hh):
+            act(cmp_out(b, hh), P(3 if hh else 2), ACT.Sign, bias=V("ts", 32 * b + 16 * hh, 32 * b + 16 * hh + 1), scale=-1.0)
+
+        def q_cmp(k):
+            quant("cmq", "cms", V("cmp", 4 * C * k, 4 * C * (k + 1)), C * k, C)
+            mm(0, C, "cq", "cs", 512, "cmq", "cms", C * k, start=k == 0, stop=k == 4, joint="rank%d" % r)
+
+        for k in range(5):
+            for b in (2 * k, 2 * k + 1):
+                if b in S_EXTRA:
+                    s_cmp(b, 0)
+                else:
+                    ts(cmp_out(b, 0), P(1), V("ts", 32 * b, 32 * b + 1), A.is_lt, 2.0, A.mult)
+            for b in (2 * k, 2 * k + 1):
+                s_cmp(b, 1)
+            if k:
+                q_cmp(k - 1)
+            if k == 1:
+                for b in range(4):
+                    mm(4 + b, C, "cq", "cs", 128 * b, "qx", "sx", 0)
+        q_cmp(4)
+        if r == 0:
+            quant("cq", "cs", V("ct", 512, 1536), 640, 256)
+
+        def f_out(b):
+            act(V("fw", 480 * b, 480 * b + C), P(4 + b))
+
+        BIG, ZERO = V("big"), V("st", 3, 4 * C, 4)
+        ZT, RHO, RR, CNT = V("col", 0, 1), V("col", 2, 3), V("col", 4, 5), V("col", 6, 7)
+        f_out(0)
+        ts(BIG, P(0), TH, A.is_lt, SH, A.subtract)
+        act(V("st", 2, 4 * C, 4), BIG, ACT.Identity, bias=SH, acc=CNT)
+        tt(V("wv"), P(0), BIG, A.add)
+        f_out(1)
+        lin(RHO, CNT, -1.0 / 512, RB)
+        op("v", lambda: g.vector.tensor_reduce(T.col[:, 0:1], T.wv[:, 0:C], AxisListType.X, A.min), V("wv")[1], ZT[1])
+        ts(V("eqs"), V("wv"), ZT, A.is_equal, SGS, A.mult)
+        act(V("ne"), V("wv"), ACT.Sign, bias=ZT, scale=-1.0)
+        scan(V("pre"), V("eqs"), ZERO, INIT, A.add, A.add)
+        ts(RR, V("pre", C - 1, C), UP, A.mult, RHO, A.add)
+        tt(V("yy"), V("pre"), V("ne"), A.subtract)
+        ts(V("st", 0, 4 * C, 4), V("yy"), RR, A.is_lt)
+        quant("stq", "sts", V("st"))
+        mm(2, C, "cq", "cs", 768, "stq", "sts", 0)
+        mm(1, C, "cq", "cs", 640, "stq", "sts", 0)
+        if r == 0:
+            lin(V("na"), ZERO, 1.0, TA)
+            act(PAR, cf(5), ACT.Abs, bias=ODD, scale=-1.0)
+            lin(Q16, QQ, 16.0, 0.0)
+            lin(GO, ODD, GRP, -1.0)
+            lin(cf(21), ODD, -16.0, 32.0)
+            lin(V("dw"), V("small", 32, 64), 1.0, QQ)
+            lin(V("tp", 0, 32), V("small", 64, 96), 1.0, QQ)
+            lin(C336, PAR, 336.0, Q16)
+            lin(C176, PAR, 176.0, Q16)
+            lin(cf(22), QQ, -1.0, cf(21))
+            lin(BQ, C176, 1.0, cf(22))
+        f_out(2)
+        f_out(3)
+        if r == 0:
+            ts(V("lj"), V("small", 0, 4), C336, A.add, 671.0, A.min)
+            ts(V("lk", 0, 1), ODD, 16.0, A.mult, 672.0, A.add)
+            ts(V("lc", 0, 1), C176, 12.0, A.add, 351.0, A.min)
+            ts(V("lbt", 0, 7), V("small", 8, 15), GO, A.is_equal, BQ, A.mult)
+            ts(V("lbt", 7, 9), V("small", 16, 18), BQ, A.add)
+
+        scan(V("nb"), P(2), V("na"), -160.0, A.add, A.add)
+        if r == 0:
+            ts(V("lb", 0, 9), V("lbt", 0, 9), QQ, A.add, 383.0, A.min)
+        scan(V("pj", 17, 17 + C), P(1), V("nb"), -160.0, A.add, A.max)
+        ts(V("pj", 353, 385), V("idr", 0, 32), 0.0, A.mult, V("pj", 16 + C, 17 + C), A.add)
+        tr2("tb", 672, "pj", 17, C, 32)
+        tr2("tb", 0, "pj", 16, C)
+        lin(V("kap"), ind(V("tb", 672, 1376), V("lk", 0, 1)), 1.0, -2528.0)
+        lin(V("nb1", 0, 32), ind(V("tb", 672, 1376), V("lj", 0, 2)), 1024.0, -1184.0)
+        lin(V("nb1", 32, 64), ind(V("tb", 672, 1376), V("lj", 2, 4)), 1024.0, V("kap", 0, 1))
+        ts(V("na1"), ind(V("tb", 0, 672), V("lj")), 1025.0, A.mult)
+        tt(V("nx"), V("na1"), V("nb1"), A.subtract)
+        tt(V("ny", 0, 32), V("nx", 32, 64), V("nx", 0, 32), A.subtract)
+        tt(V("ny", 32, 64), V("nx", 0, 32), V("dw"), A.min)
+        tt(V("ny", 64, 96), V("ny", 0, 32), V("ny", 32, 64), A.min)
+        cp(V("osc1"), V("ny", 64, 96))
+        scatter(V("rw"), V("osc1", 0, 20), V("pj", 16, 16 + C))
+        tt(V("pr", 16, 16 + K), V("rw", 0, K), V("rw", K, 2 * K), A.min)
+        tr2("tp", 32, "pr", 16, K)
+        ts(V("ob"), ind(V("tp"), V("lb", 0, 9)), 160.0, A.add)
+        for src, dst in ((2, 3), (1, 2), (1, 3), (0, 1), (0, 2), (0, 3)):
+            cp(V("ob", 32 * src, 32 * src + 32, quad=dst), V("ob", 112, 144, quad=src))
+
+        def blk(s):
+            return V("ob", 16 * s, 16 * s + 10)
+
+        src = V("rw", 0, K)
+        for s in range(6, 1, -1):
+            dst = V("cb" if s % 2 else "ca")
+            act(dst, ind(src, blk(s)))
+            src = dst
+        cp(V("la"), ind(V("idr"), blk(1)))
+        cp(V("lr", 16, 16 + K), ind(V("la"), blk(0)))
+        tr2("tl", 0, "lr", 16, K)
+        ts(V("oll"), ind(V("tl"), V("lc", 0, 1)), 0.0, A.add)
+        cp(V("cr", 16, 16 + K), ind(src, V("oll", 0, 10)))
+        tr2("tc", 0, "cr", 16, K)
+        ts(V("ocl"), ind(V("tc"), V("lc", 0, 1)), 160.0, A.add)
+        PL = V("ocl", 0, 10)
+
+        for b in range(4):
+            (cp if b < 2 else act)(V("z", b, 4 * K, 4), ind(V("fw", 480 * b, 480 * b + C), PL))
+        quant("qz", "sz", V("z"))
+        for b in range(4):
+            mm(4 + b, K, "qw", "sw", 128 * b, "qz", "sz", 0)
+        for b in range(4):
+            if b % 2:
+                ts(V("h", b, 4 * K, 4), P(4 + b, K), 0.0, A.max, 0.015625, A.mult)
+            else:
+                act(V("h", b, 4 * K, 4), P(4 + b, K), ACT.Relu, scale=0.015625)
+        quant("outq%d" % r, "outs%d" % r, V("h"))
+
+        pieces = pieces_of(core, partner, topo)
+
+        def send(r=r, pieces=pieces):
+            for call in sorted(set(p[5] for p in pieces)):
+                tx = []
+                for p in pieces:
+                    if p[5] == call:
+                        rid, pid = topo.addr(p[0], core)
+                        tx.append(RemoteDMATransfer(dst_ids=[DstId(rid=rid, pnc=pid)], dma_engine_mask=p[4], remote_sem=T.sem["hop%d" % r],
+                                                    src=side(T, "out", r, p), dst=side(T, "hop", r, p)))
+                g.remote_dma_fused(tx, local_sem=T.sem.sent)
+
+        op("g", send, regs(V("outq%d" % r), V("outs%d" % r)), [])
+        sent += sum(popcount(p[4]) for p in pieces)
+
+        scatter(V("ur", 16, 16 + C), PL, V("thr"))
+        tr2("tu", 0, "ur", 16, C)
+        cp(V("ou"), ind(V("tu"), V("lj", 2, 4)))
+        if r == ROUNDS - 1:
+            lin(V("plb"), V("cr", 16, 16 + K), 1.0, 160.0)
+            dma("y", T.pl[:], T.plb[12:128:16, :], V("plb")[1], [], must=True)
+        if r == 0:
+            quant("qv", "sv", V("vin"))
+
+        arrive = sum(popcount(topo.mask(p[0], core)) for p in pieces_of(partner, core, topo))
+        for b in range(4):
+            mm(4 + b, K, "cq", "cs", 128 * b, "landq%d" % r, "lands%d" % r, 0, ext=[(T.sem["arr%d" % r], arrive)] if b == 0 else ())
+        for b in range(4):
+            tt(V("fw", 480 * b + C, 480 * b + 480), P(4 + b, K), V("z", b, 4 * K, 4), A.add)
+            if b < 2:
+                act(V("xn", b, 4 * C, 4), ind(V("fw", 480 * b, 480 * b + 480), V("ou", 0, 20)))
+        act(V("xn", 2 * C + 2, 4 * C, 4), ind(V("fw", 960, 1440), V("ou", 10, 20)))
+        cp(V("xn", 3, 4 * C, 4), ind(V("fw", 1440, 1920), V("ou", 0, 20)))
+        cp(V("xn", 2, 2 * C, 4), ind(V("fw", 960, 1440), V("ou", 0, 10)))
+        quant("qx", "sx", V("xn"))
+
+    mm(0, K, "qv", "sv", 0, "qx", "sx", 0)
+    mm(1, K, "qv", "sv", 0, "qx", "sx", K)
+    dma("y", T.oc[:], T.qx[:].bitcast(dt.uint8), V("qx")[1], [], must=True)
+    for k in range(4):
+        dma("s" if k < 2 else "y", T.osc[4 * k:4 * k + 4, :], T.sx[32 * k:32 * k + 4, :], V("sx")[1], [], must=True)
+    cp(V("yb", 0, K), P(0, K))
+    act(V("yb", K, C), P(1, K))
+    dma("s", T.y[:], T.yb[:], V("yb")[1], [], must=True)
+
+    emit(g, T, ops)
+    g.wait_ge(T.sem.sent, sent)

@@ -10,10 +10,10 @@ SIZES = {
          "nb": C, "pj": 400, "tb": 1376, "rw": 640, "pr": 192, "tp": 384,
          "ca": K, "cb": K, "la": K, "lr": 192, "tl": 352, "cr": 192, "tc": 352,
          "fw": 4 * 480, "z": 4 * K, "h": 4 * K, "xn": 4 * C},
-    F32: {"cf": 32, "small": 128, "lbt": 16, "dw": 32, "thr": K, "ts": C, "big": C, "kap": 16, "col": 8,
-          "na1": 64, "nb1": 64, "nx": 64, "ny": 96, "ur": 352, "tu": 672, "plb": K, "yb": C},
+    F32: {"cf": 32, "small": 192, "lbt": 16, "dw": 32, "thr": K, "ts": C, "big": C, "kap": 16, "col": 8,
+          "nb1": 64, "nx": 64, "ny": 96, "ur": 352, "tu": 672, "plb": K, "yb": C},
     I32: {"ci": 8, "lui": 16},
-    U16: {"lu": 16, "lj": 4, "lc": 2, "lk": 2, "lb": 10, "osc1": 32, "ob": 144, "oll": 16, "ocl": 16, "ou": 32},
+    U16: {"lu": 16, "lj": 4, "lc": 2, "lk": 2, "lb": 4, "osc1": 32, "ob": 144, "oll": 16, "ocl": 16, "ou": 32},
     X4: {"qx": C, "qu": 128, "qu2": 256, "qv": 128, "qw": 512, "cq": 896, "cmq": 5 * C, "stq": C, "qz": K},
     U8: {"sx": C, "su": 128, "su2": 256, "sv": 128, "sw": 512, "cs": 896, "cms": 5 * C, "sts": C, "sz": K},
 }
@@ -25,13 +25,14 @@ for _r in range(ROUNDS):
 for _b in range(8):
     SCRATCH["ps%d" % _b] = ("psum", [128, 512], F32)
 
-POOL = {"v": 40, "s": 34, "t": 18, "g": 36, "d": 14}
+POOL = {"v": 40, "s": 34, "t": 18, "g": 34, "d": 16}
 SEMAPHORES = ["%s_%d" % (q, i) for q in POOL for i in range(POOL[q])]
 SEMAPHORES += ["hop%d" % r for r in range(ROUNDS)] + ["arr%d" % r for r in range(ROUNDS)] + ["sent"]
 
 A = AluOpType
 ACT = ActivationFunctionType
-S_EXTRA = (0, 4, 6)
+ORDER = "e0 e1 o0 o1 v2 t0 v3 o2 o3 v4 q0 f0 v5 o4 o5 q1 e6 o6 o7 v7 q2 v8 v9 o8 o9 q3 q4"
+UPDATE = (("s", 0, 0), ("s", 1, 0), ("v", 2, 0), ("v", 3, 0), ("s", 0, 1), ("s", 1, 1), ("v", 3, 1), ("v", 4, 0), ("s", 2, 1), ("v", 4, 1))
 
 
 def popcount(m):
@@ -150,9 +151,9 @@ def rank_program(g, core, T, topo):
         return
     ops = []
 
-    def V(name, lo=0, hi=None, step=1, quad=None):
+    def V(name, lo=0, hi=None, step=1, quad=None, tall=1):
         hi = T[name].shape[1] if hi is None else hi
-        p0, p1 = (0, 128) if quad is None else (32 * quad, 32 * quad + 32)
+        p0, p1 = (0, 128) if quad is None else (32 * quad, 32 * (quad + tall))
         cols = slice(lo, hi) if step == 1 else slice(lo, hi, step)
         ap = T[name][:, cols] if quad is None else T[name][p0:p1, cols]
         return (ap, [(name, lo, hi, step, p0, p1)])
@@ -190,9 +191,9 @@ def rank_program(g, core, T, topo):
     def tr(out, a):
         op("v", lambda: g.vector.transpose(out[0], a[0]), a[1], out[1])
 
-    def tr2(out, o0, row, r0, n, more=0):
+    def tr2(out, o0, row, r0, n):
         tr(V(out, o0, o0 + n), V(row, r0, r0 + n))
-        tr(V(out, o0 + n, o0 + 2 * n + 32 + more), V(row, r0 - 16, r0 + n + 16 + more))
+        tr(V(out, o0 + n, o0 + 2 * n + 32), V(row, r0 - 16, r0 + n + 16))
 
     def scan(out, d0, d1, init, o0, o1):
         op("v", lambda: g.vector.tensor_tensor_scan(out[0], d0[0], d1[0], val(init), o0, o1), regs(d0, d1, init), out[1])
@@ -245,7 +246,7 @@ def rank_program(g, core, T, topo):
 
     dma("s", T.uin[:], T.u[:], [], V("uin")[1])
     dma("y", T.xin[:], T.x[:], [], V("xin")[1])
-    dma("y", T.qw[:].bitcast(dt.uint8), T.wc[:], [], V("qw")[1])
+    dma("y", T.qw[:].bitcast(dt.uint8), T.wc[:], V("xin")[1], V("qw")[1])
     dma("y", T.sw[:], T.ws[:], [], V("sw")[1])
     dma("y", T.vin[:], T.v[:], [], V("vin")[1])
 
@@ -264,32 +265,31 @@ def rank_program(g, core, T, topo):
     fill("st", 3, 4 * C, 0, 4)
     fill("st", 1, 4 * C, 0, 4)
     iota(V("small", 0, 4), [[-8, 2], [256, 2]], 8)
-    iota(V("small", 8, 16), [[1, 8]], 0)
     iota(V("small", 16, 18), [[16, 2]], 0)
     iota(V("small", 32, 64), [[16, 32]], C)
     iota(V("small", 64, 96), [[16, 32]], -K)
+    iota(V("small", 96, 192), [[0, 6], [16, 16]], 0)
     fill("pj", 0, 17, -K)
-    fill("pj", 337, 353, 0)
+    fill("pj", 337, 354, 0)
     iota(V("idr"), [[1, K]], 0)
     for name, n in (("pr", K), ("lr", K), ("cr", K), ("ur", C)):
         fill(name, 0, 16, 0)
         fill(name, 16 + n, T[name].shape[1], 0)
     iota(V("thr"), [[1, K]], C)
 
-    ts(ci(1), ci(0), 4, A.arith_shift_right)
     ts(ci(2), ci(0), 15, A.bitwise_and)
     ts(ci(3), ci(0), 3, A.arith_shift_right, 1, A.bitwise_and)
     ts(ci(4), ci(0), 4, A.arith_shift_right, 1, A.bitwise_and)
     ts(ci(5), ci(0), 1, A.bitwise_and)
     ts(ci(6), ci(0), 2, A.arith_shift_right, 3, A.bitwise_and)
     cp(V("lu"), V("lui"))
-    cp(V("cf", 0, 7), V("ci", 0, 7))
+    cp(V("cf", 2, 7), V("ci", 2, 7))
     for b in range(4):
         quant("cq", "cs", V("e0", 4 - b, 516 - b), 128 * b, 128)
-    GRP, QQ, UP, ODD = cf(1), cf(2), cf(3), cf(4)
-    SG, TH, RB, SGS, INIT, TA, PAR, Q16, C336, C176, GO, BQ = [cf(k) for k in range(8, 20)]
+    QQ, UP, ODD = cf(2), cf(3), cf(4)
+    SG, TH, RB, SGS, INIT, TA, PAR, Q16, C336, C176, QN, BQ = [cf(k) for k in range(8, 20)]
     SH = cf(23)
-    n0, n1 = 32.0 * len(S_EXTRA), 320.0
+    n0, n1 = 32.0 * ORDER.count("e"), 320.0
     lin(SG, UP, -2.0, 1.0)
     lin(cf(20), ODD, (n0 - n1) / 1024, (319.5 - n0) / 1024)
     lin(RB, UP, 160.0 / 512, 0.0)
@@ -307,6 +307,7 @@ def rank_program(g, core, T, topo):
     op("s", lambda: g.scalar.activation(T.su2[:, 0:256], T.su[:, 0:128].indirect(T.lu[:, 0:16]), ACT.Copy),
        regs(V("su"), V("lu")), V("su2")[1])
     quant("qx", "sx", V("xin"))
+    quant("cq", "cs", V("ct", 0, 512), 512, 128)
 
     sent = 0
     for r in range(ROUNDS):
@@ -315,39 +316,43 @@ def rank_program(g, core, T, topo):
         iota(V("ur", 16, 16 + C), [[1, C]], 0)
         mm(0, 128, "qu", "su", 0, "qx", "sx", 0)
         mm(2, C, "qu2", "su2", 0, "qx", "sx", 0)
-        mm(4, C - 128, "qu", "su", 0, "qx", "sx", 128)
-        mm(3, C, "qu2", "su2", 128, "qx", "sx", 0)
         mm(1, C, "qu2", "su2", 0, "qx", "sx", 0)
+        mm(3, C, "qu2", "su2", 128, "qx", "sx", 0)
+        mm(4, C - 128, "qu", "su", 0, "qx", "sx", 128)
         tr(V("ts", 0, 128), P(0, 128))
-        tr(V("ts", 128, C), P(4, C - 128))
-        if r == 0:
-            quant("cq", "cs", V("ct", 0, 512), 512, 128)
 
         def cmp_out(b, hh):
             k = b // 2
             return V("cmp", 4 * C * k + 2 * (b % 2) + hh, 4 * C * (k + 1), 4)
 
         def s_cmp(b, hh):
-            act(cmp_out(b, hh), P(3 if hh else 2), ACT.Sign, bias=V("ts", 32 * b + 16 * hh, 32 * b + 16 * hh + 1), scale=-1.0)
+            s = V("ts", 32 * b + 16 * hh, 32 * b + 16 * hh + 1)
+            if b < 9:
+                act(cmp_out(b, hh), P(3 if hh else 2), ACT.Sign, bias=s, scale=-1.0)
+            else:
+                for lo in (0, K):
+                    act(V("cmp", 16 * C + 4 * lo + 3, 16 * C + 4 * lo + 4 * K, 4), V("ps3", lo, lo + K), ACT.Sign, bias=s, scale=-1.0)
 
         def q_cmp(k):
-            quant("cmq", "cms", V("cmp", 4 * C * k, 4 * C * (k + 1)), C * k, C)
+            for lo, n in (((0, C),) if k < 4 else ((0, K), (K, K))):
+                quant("cmq", "cms", V("cmp", 4 * (C * k + lo), 4 * (C * k + lo + n)), C * k + lo, n)
             mm(0, C, "cq", "cs", 512, "cmq", "cms", C * k, start=k == 0, stop=k == 4, joint="rank%d" % r)
 
-        for k in range(5):
-            for b in (2 * k, 2 * k + 1):
-                if b in S_EXTRA:
-                    s_cmp(b, 0)
-                else:
-                    ts(cmp_out(b, 0), P(1), V("ts", 32 * b, 32 * b + 1), A.is_lt, 2.0, A.mult)
-            for b in (2 * k, 2 * k + 1):
+        for step in ORDER.split():
+            kind, b = step[0], int(step[1])
+            if kind == "e":
+                s_cmp(b, 0)
+            elif kind == "o":
                 s_cmp(b, 1)
-            if k:
-                q_cmp(k - 1)
-            if k == 1:
+            elif kind == "v":
+                ts(cmp_out(b, 0), P(1), V("ts", 32 * b, 32 * b + 1), A.is_lt, 2.0, A.mult)
+            elif kind == "q":
+                q_cmp(b)
+            elif kind == "t":
+                tr(V("ts", 128, C), P(4, C - 128))
+            else:
                 for b in range(4):
                     mm(4 + b, C, "cq", "cs", 128 * b, "qx", "sx", 0)
-        q_cmp(4)
         if r == 0:
             quant("cq", "cs", V("ct", 512, 1536), 640, 256)
 
@@ -357,78 +362,87 @@ def rank_program(g, core, T, topo):
         BIG, ZERO = V("big"), V("st", 3, 4 * C, 4)
         ZT, RHO, RR, CNT = V("col", 0, 1), V("col", 2, 3), V("col", 4, 5), V("col", 6, 7)
         f_out(0)
-        ts(BIG, P(0), TH, A.is_lt, SH, A.subtract)
+        for lo in (0, K):
+            ts(V("big", lo, lo + K), V("ps0", lo, lo + K), TH, A.is_lt, SH, A.subtract)
         act(V("st", 2, 4 * C, 4), BIG, ACT.Identity, bias=SH, acc=CNT)
-        tt(V("wv"), P(0), BIG, A.add)
+        for lo in (0, K):
+            tt(V("wv", lo, lo + K), V("ps0", lo, lo + K), V("big", lo, lo + K), A.add)
         f_out(1)
         lin(RHO, CNT, -1.0 / 512, RB)
         op("v", lambda: g.vector.tensor_reduce(T.col[:, 0:1], T.wv[:, 0:C], AxisListType.X, A.min), V("wv")[1], ZT[1])
         ts(V("eqs"), V("wv"), ZT, A.is_equal, SGS, A.mult)
         act(V("ne"), V("wv"), ACT.Sign, bias=ZT, scale=-1.0)
         scan(V("pre"), V("eqs"), ZERO, INIT, A.add, A.add)
-        ts(RR, V("pre", C - 1, C), UP, A.mult, RHO, A.add)
-        tt(V("yy"), V("pre"), V("ne"), A.subtract)
-        ts(V("st", 0, 4 * C, 4), V("yy"), RR, A.is_lt)
-        quant("stq", "sts", V("st"))
+        lin(RR, V("pre", C - 1, C), UP, RHO)
+        for lo in (0, K):
+            tt(V("yy", lo, lo + K), V("pre", lo, lo + K), V("ne", lo, lo + K), A.subtract)
+        for lo in (0, K):
+            ts(V("st", 4 * lo, 4 * (lo + K), 4), V("yy", lo, lo + K), RR, A.is_lt)
+        for lo in (0, K):
+            quant("stq", "sts", V("st", 4 * lo, 4 * (lo + K)), lo, K)
         mm(2, C, "cq", "cs", 768, "stq", "sts", 0)
         mm(1, C, "cq", "cs", 640, "stq", "sts", 0)
         if r == 0:
             lin(V("na"), ZERO, 1.0, TA)
             act(PAR, cf(5), ACT.Abs, bias=ODD, scale=-1.0)
             lin(Q16, QQ, 16.0, 0.0)
-            lin(GO, ODD, GRP, -1.0)
+            lin(QN, QQ, -1.0 / 1024, 0.0)
             lin(cf(21), ODD, -16.0, 32.0)
-            lin(V("dw"), V("small", 32, 64), 1.0, QQ)
             lin(V("tp", 0, 32), V("small", 64, 96), 1.0, QQ)
             lin(C336, PAR, 336.0, Q16)
             lin(C176, PAR, 176.0, Q16)
             lin(cf(22), QQ, -1.0, cf(21))
+            lin(V("dw"), V("small", 32, 64), -1.0 / 1024, QN)
             lin(BQ, C176, 1.0, cf(22))
         f_out(2)
         f_out(3)
         if r == 0:
             ts(V("lj"), V("small", 0, 4), C336, A.add, 671.0, A.min)
-            ts(V("lk", 0, 1), ODD, 16.0, A.mult, 672.0, A.add)
+            ts(V("lk", 0, 1), ODD, 16.0, A.mult)
             ts(V("lc", 0, 1), C176, 12.0, A.add, 351.0, A.min)
-            ts(V("lbt", 0, 7), V("small", 8, 15), GO, A.is_equal, BQ, A.mult)
-            ts(V("lbt", 7, 9), V("small", 16, 18), BQ, A.add)
+            ts(V("ob", 48, 144), V("small", 96, 192), QQ, A.add)
 
         scan(V("nb"), P(2), V("na"), -160.0, A.add, A.add)
         if r == 0:
-            ts(V("lb", 0, 9), V("lbt", 0, 9), QQ, A.add, 383.0, A.min)
+            ts(V("lbt", 0, 1), ODD, BQ, A.mult)
+            ts(V("lbt", 1, 3), V("small", 16, 18), BQ, A.add)
         scan(V("pj", 17, 17 + C), P(1), V("nb"), -160.0, A.add, A.max)
-        ts(V("pj", 353, 385), V("idr", 0, 32), 0.0, A.mult, V("pj", 16 + C, 17 + C), A.add)
-        tr2("tb", 672, "pj", 17, C, 32)
-        tr2("tb", 0, "pj", 16, C)
-        lin(V("kap"), ind(V("tb", 672, 1376), V("lk", 0, 1)), 1.0, -2528.0)
-        lin(V("nb1", 0, 32), ind(V("tb", 672, 1376), V("lj", 0, 2)), 1024.0, -1184.0)
-        lin(V("nb1", 32, 64), ind(V("tb", 672, 1376), V("lj", 2, 4)), 1024.0, V("kap", 0, 1))
-        ts(V("na1"), ind(V("tb", 0, 672), V("lj")), 1025.0, A.mult)
-        tt(V("nx"), V("na1"), V("nb1"), A.subtract)
+        if r == 0:
+            ts(V("lb", 0, 3), V("lbt", 0, 3), QQ, A.add, 383.0, A.min)
+        lin(V("pj", 368, 400), V("st", 3, 128, 4), 1.0, V("pj", 16 + C, 17 + C))
+        tr(V("tb", 0, C), V("pj", 16, 16 + C))
+        tr(V("tb", 672, 704), V("pj", 368, 400))
+        tr(V("tb", C, 672), V("pj", 0, 352))
+        tr2("tb", 704, "pj", 17, C)
+        lin(V("kap"), ind(V("tb", 672, 704), V("lk", 0, 1)), -1.0 / 1024, 2528.0 / 1024)
+        lin(V("nb1", 0, 32), ind(V("tb", 0, 672), V("lj", 0, 2)), 1025.0 / 1024, 1184.0 / 1024)
+        lin(V("nb1", 32, 64), ind(V("tb", 0, 672), V("lj", 2, 4)), 1025.0 / 1024, V("kap", 0, 1))
+        tt(V("nx"), ind(V("tb", 704, 1376), V("lj")), V("nb1"), A.subtract)
         tt(V("ny", 0, 32), V("nx", 32, 64), V("nx", 0, 32), A.subtract)
-        tt(V("ny", 32, 64), V("nx", 0, 32), V("dw"), A.min)
-        tt(V("ny", 64, 96), V("ny", 0, 32), V("ny", 32, 64), A.min)
-        cp(V("osc1"), V("ny", 64, 96))
+        tt(V("ny", 32, 64), V("nx", 0, 32), V("dw"), A.max)
+        tt(V("ny", 64, 96), V("ny", 0, 32), V("ny", 32, 64), A.max)
+        ts(V("osc1"), V("ny", 64, 96), -1024.0, A.mult)
         scatter(V("rw"), V("osc1", 0, 20), V("pj", 16, 16 + C))
         tt(V("pr", 16, 16 + K), V("rw", 0, K), V("rw", K, 2 * K), A.min)
         tr2("tp", 32, "pr", 16, K)
-        ts(V("ob"), ind(V("tp"), V("lb", 0, 9)), 160.0, A.add)
-        for src, dst in ((2, 3), (1, 2), (1, 3), (0, 1), (0, 2), (0, 3)):
-            cp(V("ob", 32 * src, 32 * src + 32, quad=dst), V("ob", 112, 144, quad=src))
+        ts(V("ob", 0, 48), ind(V("tp"), V("lb", 0, 3)), 160.0, A.add)
+        for src, up, tall in ((0, 1, 1), (1, 1, 1), (2, 1, 1), (0, 3, 1), (0, 2, 2)):
+            cp(V("ob", 16 + 32 * up, 48 + 32 * up, quad=src + up, tall=tall), V("ob", 16, 48, quad=src, tall=tall))
 
-        def blk(s):
-            return V("ob", 16 * s, 16 * s + 10)
+        def both(dst, d0, src, lst, c0, n):
+            act(V(dst, d0, d0 + 16 * n), ind(src, V(lst, c0, c0 + n)))
+            cp(V(dst, d0 + 16 * n, d0 + K), ind(src, V(lst, c0 + n, c0 + 10)))
 
-        src = V("rw", 0, K)
-        for s in range(6, 1, -1):
-            dst = V("cb" if s % 2 else "ca")
-            act(dst, ind(src, blk(s)))
-            src = dst
-        cp(V("la"), ind(V("idr"), blk(1)))
-        cp(V("lr", 16, 16 + K), ind(V("la"), blk(0)))
+        act(V("ca"), ind(V("rw", 0, K), V("ob", 0, 10)))
+        both("cb", 0, V("ca"), "ob", 64, 6)
+        both("la", 0, V("idr"), "ob", 128, 4)
+        both("ca", 0, V("cb"), "ob", 48, 6)
+        both("lr", 16, V("la"), "ob", 112, 4)
+        both("cb", 0, V("ca"), "ob", 96, 6)
         tr2("tl", 0, "lr", 16, K)
+        both("ca", 0, V("cb"), "ob", 80, 6)
         ts(V("oll"), ind(V("tl"), V("lc", 0, 1)), 0.0, A.add)
-        cp(V("cr", 16, 16 + K), ind(src, V("oll", 0, 10)))
+        both("cr", 16, V("ca"), "oll", 0, 4)
         tr2("tc", 0, "cr", 16, K)
         ts(V("ocl"), ind(V("tc"), V("lc", 0, 1)), 160.0, A.add)
         PL = V("ocl", 0, 10)
@@ -474,21 +488,22 @@ def rank_program(g, core, T, topo):
             mm(4 + b, K, "cq", "cs", 128 * b, "landq%d" % r, "lands%d" % r, 0, ext=[(T.sem["arr%d" % r], arrive)] if b == 0 else ())
         for b in range(4):
             tt(V("fw", 480 * b + C, 480 * b + 480), P(4 + b, K), V("z", b, 4 * K, 4), A.add)
-            if b < 2:
-                act(V("xn", b, 4 * C, 4), ind(V("fw", 480 * b, 480 * b + 480), V("ou", 0, 20)))
-        act(V("xn", 2 * C + 2, 4 * C, 4), ind(V("fw", 960, 1440), V("ou", 10, 20)))
-        cp(V("xn", 3, 4 * C, 4), ind(V("fw", 1440, 1920), V("ou", 0, 20)))
-        cp(V("xn", 2, 2 * C, 4), ind(V("fw", 960, 1440), V("ou", 0, 10)))
-        quant("qx", "sx", V("xn"))
+        for e, b, hf in UPDATE:
+            if b < 4:
+                (cp if e == "v" else act)(V("xn", 2 * C * hf + b, 2 * C * (hf + 1), 4), ind(V("fw", 480 * b, 480 * b + 480), V("ou", 10 * hf, 10 * hf + 10)))
+            else:
+                quant("qx", "sx", V("xn", 2 * C * hf, 2 * C * (hf + 1)), K * hf, K)
 
     mm(0, K, "qv", "sv", 0, "qx", "sx", 0)
     mm(1, K, "qv", "sv", 0, "qx", "sx", K)
-    dma("y", T.oc[:], T.qx[:].bitcast(dt.uint8), V("qx")[1], [], must=True)
+    for lo in (0, K):
+        dma("y", T.oc[:, 4 * lo:4 * (lo + K)], T.qx[:, lo:lo + K].bitcast(dt.uint8), V("qx", lo, lo + K)[1], [], must=True)
+    cp(V("yb", 0, K), P(0, K))
+    dma("y", T.y[:, 0:K], T.yb[:, 0:K], V("yb", 0, K)[1], [], must=True)
     for k in range(4):
         dma("s" if k < 2 else "y", T.osc[4 * k:4 * k + 4, :], T.sx[32 * k:32 * k + 4, :], V("sx")[1], [], must=True)
-    cp(V("yb", 0, K), P(0, K))
     act(V("yb", K, C), P(1, K))
-    dma("s", T.y[:], T.yb[:], V("yb")[1], [], must=True)
+    dma("s", T.y[:, K:C], T.yb[:, K:C], V("yb", K, C)[1], [], must=True)
 
     emit(g, T, ops)
     g.wait_ge(T.sem.sent, sent)

@@ -1,21 +1,22 @@
 from concourse.bass import DstId, RemoteDMATransfer
-from concourse.mybir import dt, AluOpType, AxisListType, ActivationFunctionType
+from concourse.mybir import dt, AluOpType, ActivationFunctionType
 
 C, K, ROUNDS = 320, 160, 3
 STEP = [1, 2, 4]
+BIG = 1024
+CX = C + 32
 X4, U8, U16, BF, F32, I32 = "float8_e4m3fn_x4", "uint8", "uint16", "bfloat16", "float32", "int32"
 SIZES = {
-    BF: {"xin": 4 * C, "uin": 512, "vin": 512, "brow": 256, "e0": 520, "ct": 1536, "na": C, "idr": K,
-         "cmp": 20 * C, "st": 4 * C, "eqs": C, "ne": C, "pre": C, "yy": C, "wv": C,
-         "nb": C, "pj": 400, "tb": 1376, "rw": 640, "pr": 192, "tp": 384,
-         "ca": K, "cb": K, "la": K, "lr": 192, "tl": 352, "cr": 192, "tc": 352,
-         "fw": 4 * 480, "z": 4 * K, "h": 4 * K, "xn": 4 * C},
-    F32: {"cf": 32, "small": 192, "lbt": 16, "dw": 32, "thr": K, "ts": C, "big": C, "kap": 16, "col": 8,
-          "nb1": 64, "nx": 64, "ny": 96, "ur": 352, "tu": 672, "plb": K, "yb": C},
+    BF: {"xin": 4 * C, "uin": 512, "vin": 512, "e0": 520, "ct": 1536, "row0": 192, "msk": 64, "keep": 640, "cmp": 3840,
+         "rs": 1792, "em": C, "et": C, "na": CX, "nb": CX + 4, "pj": 384, "tb": 2 * CX, "rw": 992, "tp": 352,
+         "cr": 192, "tc": 352, "ca": K, "cb": K, "c2": 192, "td": 352, "ur": 352, "tu": 672, "thr": K,
+         "fw": 4 * 480, "z": 4 * K, "z2": 4 * K, "h": 4 * K, "xn": 4 * C},
+    F32: {"cf": 16, "small": 128, "ini": 96, "tab": 96, "ts": C, "acc": 8, "ce": 20, "rmp": 32,
+          "l1": 96, "l2": 96, "l3": 64, "plb": K, "yb": C},
     I32: {"ci": 8, "lui": 16},
-    U16: {"lu": 16, "lj": 4, "lc": 2, "lk": 2, "lb": 4, "osc1": 32, "ob": 144, "oll": 16, "ocl": 16, "ou": 32},
-    X4: {"qx": C, "qu": 128, "qu2": 256, "qv": 128, "qw": 512, "cq": 896, "cmq": 5 * C, "stq": C, "qz": K},
-    U8: {"sx": C, "su": 128, "su2": 256, "sv": 128, "sw": 512, "cs": 896, "cms": 5 * C, "sts": C, "sz": K},
+    U16: {"lu": 16, "lj": 16, "lc": 4, "le": 2, "osc1": 32, "ob": 32, "orr": 64, "ocl": 16, "ou": 32},
+    X4: {"qx": C, "qu": 128, "qu2": 256, "qv": 128, "qw": 512, "cq": 896, "cmq": 1216, "qa": K, "qb": K, "qc": K, "qd": K},
+    U8: {"sx": C, "su": 128, "su2": 256, "sv": 128, "sw": 512, "cs": 896, "cms": 1216, "sa": K, "sb": K, "sc": K, "sd": K},
 }
 SCRATCH = {n: ("sbuf", [128, w], d) for d in SIZES for n, w in SIZES[d].items()}
 for _r in range(ROUNDS):
@@ -25,13 +26,19 @@ for _r in range(ROUNDS):
 for _b in range(8):
     SCRATCH["ps%d" % _b] = ("psum", [128, 512], F32)
 
-POOL = {"v": 40, "s": 34, "t": 18, "g": 34, "d": 16}
+POOL = {"v": 26, "s": 24, "t": 14, "g": 62, "d": 16}
 SEMAPHORES = ["%s_%d" % (q, i) for q in POOL for i in range(POOL[q])]
 SEMAPHORES += ["hop%d" % r for r in range(ROUNDS)] + ["arr%d" % r for r in range(ROUNDS)] + ["sent"]
 
 A = AluOpType
 ACT = ActivationFunctionType
-ORDER = "e0 e1 o0 o1 v2 t0 v3 o2 o3 v4 q0 f0 v5 o4 o5 q1 e6 o6 o7 v7 q2 v8 v9 o8 o9 q3 q4"
+KT, KC, KF1, KF2, KF3, KRP, KRN, KD = range(8)
+ADDED = ((KT, 0, 0, 1), (KD, 0, 0, -1), (KF1, 0, 0, -BIG), (KF2, 1, -1, BIG), (KF2, 1, 0, -BIG), (KF3, 1, 0, BIG), (KF3, 1, 1, -BIG))
+SUMMED = ((KT, 1, 1, 1), (KRN, 1, 1, 1), (KRN, 1, 0, -1), (KRP, 1, 0, 1), (KRP, 1, -1, -1), (KD, 1, -1, -1))
+START = {KT: -K, KC: -K, KF1: BIG, KF2: BIG + 80, KF3: BIG, KRN: 81, KD: 241}
+TILE = [896, 768, 576, 320, 0]
+ORDER = ("c00 c01 c10 c11 t s90 s91 c20 c21 m0 m1 c30 c31 s80 s81 m9 m2 c40 c41 m3 r90 m8 r91 q0 c50 c51 m4 r80 r81 c60 f m5 s70 s71 s61 q2 q4 "
+         "n0 m7 m6 r70 r71 n2 n3 r61 n1 e q3")
 UPDATE = (("s", 0, 0), ("s", 1, 0), ("v", 2, 0), ("v", 3, 0), ("s", 0, 1), ("s", 1, 1), ("v", 3, 1), ("v", 4, 0), ("s", 2, 1), ("v", 4, 1))
 
 
@@ -77,7 +84,8 @@ def relay_program(g, core, T, topo):
 def overlap(a, b):
     if a[0] != b[0] or a[2] <= b[1] or b[2] <= a[1] or a[5] <= b[4] or b[5] <= a[4]:
         return False
-    return not (a[3] == b[3] and a[3] > 1 and a[1] % a[3] != b[1] % b[3])
+    step = min(a[3], b[3])
+    return not (step > 1 and max(a[3], b[3]) % step == 0 and a[1] % step != b[1] % step)
 
 
 def emit(g, T, ops):
@@ -191,9 +199,9 @@ def rank_program(g, core, T, topo):
     def tr(out, a):
         op("v", lambda: g.vector.transpose(out[0], a[0]), a[1], out[1])
 
-    def tr2(out, o0, row, r0, n):
-        tr(V(out, o0, o0 + n), V(row, r0, r0 + n))
-        tr(V(out, o0 + n, o0 + 2 * n + 32), V(row, r0 - 16, r0 + n + 16))
+    def tr2(out, row, n):
+        tr(V(out, 0, n), V(row, 16, 16 + n))
+        tr(V(out, n, 2 * n + 32), V(row, 0, n + 32))
 
     def scan(out, d0, d1, init, o0, o1):
         op("v", lambda: g.vector.tensor_tensor_scan(out[0], d0[0], d1[0], val(init), o0, o1), regs(d0, d1, init), out[1])
@@ -214,6 +222,11 @@ def rank_program(g, core, T, topo):
 
     def lin(out, a, scale, bias):
         act(out, a, ACT.Identity, bias=bias, scale=scale)
+
+    def pick(dst, src, off):
+        q2, q1, s2, s1 = V("q" + dst), V("q" + src), V("s" + dst), V("s" + src)
+        op("v", lambda: g.vector.tensor_copy(q2[0].bitcast(dt.uint32), q1[0].bitcast(dt.uint32).indirect(off[0])), regs(q1, off), q2[1])
+        act(s2, ind(s1, off))
 
     def mm(bank, n, lq, ls, l0, rq, rs, r0, start=True, stop=True, joint=None, ext=()):
         o, a, b, c, d = V("ps%d" % bank, 0, n), V(lq, l0, l0 + 128), V(ls, l0, l0 + 128), V(rq, r0, r0 + n), V(rs, r0, r0 + n)
@@ -250,208 +263,218 @@ def rank_program(g, core, T, topo):
     dma("y", T.sw[:], T.ws[:], [], V("sw")[1])
     dma("y", T.vin[:], T.v[:], [], V("vin")[1])
 
+    QUAD, QUAD8, CC, QQ, ODD, BIT, PAR, Q16, NEGC, CB, C336, C176, CR = [cf(k) for k in range(13)]
+    INIT, NA = V("tab", 0, 1), V("tab", 32, 33)
     ms(V("e0"), 0.0)
-    ms(V("ct", 0, 512), 0.0)
+    ms(V("ct", 512, 1536), 0.0)
     iota(ci(0), [[0, 1]], 0, 1, whole=True)
     iota(V("lui"), [[16, 2], [32, 4], [0, 2]], 0, whole=True)
     mark(V("e0", 4, 516, 4), [[-1, 128]], 0, 1.0)
-    iota(V("brow", 0, 128), [[0, 2], [-2, 2], [0, 32]], 1)
-    op("g", lambda: g.affine_select(T.brow[:, 128:256], T.brow[:, 0:128], [[1, 2], [0, 32], [-1, 2]], A.is_equal, 0.0, 0, 0),
-       V("brow", 0, 128)[1], V("brow", 128, 256)[1])
-    fill("ct", 512, 1536, 0)
-    for t, row, w in ((0, 0, 1.0), (0, 8, -1.0), (2, 0, 1.0)):
-        mark(V("ct", 512 + t, 1024, 4), [[-16, 8], [0, 16]], -row, w)
-        mark(V("ct", 1024 + t, 1536, 4), [[-16, 8], [-1000, 2], [0, 8]], -16 - row, w)
-    fill("st", 3, 4 * C, 0, 4)
-    fill("st", 1, 4 * C, 0, 4)
-    iota(V("small", 0, 4), [[-8, 2], [256, 2]], 8)
-    iota(V("small", 16, 18), [[16, 2]], 0)
-    iota(V("small", 32, 64), [[16, 32]], C)
-    iota(V("small", 64, 96), [[16, 32]], -K)
-    iota(V("small", 96, 192), [[0, 6], [16, 16]], 0)
-    fill("pj", 0, 17, -K)
-    fill("pj", 337, 354, 0)
-    iota(V("idr"), [[1, K]], 0)
-    for name, n in (("pr", K), ("lr", K), ("cr", K), ("ur", C)):
-        fill(name, 0, 16, 0)
-        fill(name, 16 + n, T[name].shape[1], 0)
-    iota(V("thr"), [[1, K]], C)
-
-    ts(ci(2), ci(0), 15, A.bitwise_and)
-    ts(ci(3), ci(0), 3, A.arith_shift_right, 1, A.bitwise_and)
+    iota(V("row0", 0, 128), [[1, 4], [8, 2], [0, 16]], 0)
+    iota(V("row0", 128, 192), [[1, 32], [0, 2]], 0)
+    quant("cmq", "cms", V("ct", 512, 1536), 960, 256)
+    for k in range(5):
+        fill("cmp", 4 * (TILE[k] + 64 * k + 32) + 1, 4 * (TILE[k] + 64 * k + 64), 0, 2)
+    ts(ci(1), ci(0), 5, A.arith_shift_right)
+    ts(ci(2), ci(0), 31, A.bitwise_and)
+    ts(ci(3), ci(0), 15, A.bitwise_and)
     ts(ci(4), ci(0), 4, A.arith_shift_right, 1, A.bitwise_and)
     ts(ci(5), ci(0), 1, A.bitwise_and)
-    ts(ci(6), ci(0), 2, A.arith_shift_right, 3, A.bitwise_and)
     cp(V("lu"), V("lui"))
-    cp(V("cf", 2, 7), V("ci", 2, 7))
-    for b in range(4):
-        quant("cq", "cs", V("e0", 4 - b, 516 - b), 128 * b, 128)
-    QQ, UP, ODD = cf(2), cf(3), cf(4)
-    SG, TH, RB, SGS, INIT, TA, PAR, Q16, C336, C176, QN, BQ = [cf(k) for k in range(8, 20)]
-    SH = cf(23)
-    n0, n1 = 32.0 * ORDER.count("e"), 320.0
-    lin(SG, UP, -2.0, 1.0)
-    lin(cf(20), ODD, (n0 - n1) / 1024, (319.5 - n0) / 1024)
-    lin(RB, UP, 160.0 / 512, 0.0)
-    lin(SGS, UP, -2.0 / 512, 1.0 / 512)
-    lin(INIT, UP, 321.0 / 512, -161.0 / 512)
-    act(TA, cf(6), ACT.Relu, bias=-2.0)
-    lin(TH, cf(20), SG, 0.0)
-    for a in range(4):
-        lin(V("ct", 128 * a, 128 * a + 128, quad=a), V("brow", 128, 256, quad=a), 2.0 ** -10, 0.0)
-    lin(SH, TH, 1.0, 160.5 / 1024)
+    cp(QUAD, ci(1))
+    cp(V("cf", 2, 6), V("ci", 2, 6))
+    lin(QUAD8, QUAD, 1.0, 8.0)
+    lin(NEGC, CC, -1.0, 0.0)
+    act(PAR, BIT, ACT.Abs, bias=ODD, scale=-1.0)
+    lin(Q16, QQ, 16.0, 0.0)
+    lin(CB, PAR, 16.0 - CX, Q16)
+    lin(C336, PAR, 336.0, Q16)
+    lin(C176, PAR, 176.0, Q16)
+    lin(CR, ODD, -16.0, C176)
+    lin(V("em"), V("e0", 0, C), 0.0, 0.0)
+    lin(V("keep", 0, C), V("e0", 0, C), 0.0, 1.0)
+    lin(V("keep", C, 2 * C), V("e0", 0, C), 0.0, 1.0)
 
     quant("qu", "su", V("uin"))
     op("v", lambda: g.vector.tensor_copy(T.qu2[:, 0:256].bitcast(dt.uint32), T.qu[:, 0:128].bitcast(dt.uint32).indirect(T.lu[:, 0:16])),
        regs(V("qu"), V("lu")), V("qu2")[1])
-    op("s", lambda: g.scalar.activation(T.su2[:, 0:256], T.su[:, 0:128].indirect(T.lu[:, 0:16]), ACT.Copy),
-       regs(V("su"), V("lu")), V("su2")[1])
-    quant("qx", "sx", V("xin"))
-    quant("cq", "cs", V("ct", 0, 512), 512, 128)
+    act(V("su2"), ind(V("su"), V("lu")))
+    for b in range(4):
+        quant("cq", "cs", V("e0", 4 - b, 516 - b), 128 * b, 128)
+    for t in range(4):
+        ts(V("ct", t, 512, 4), V("row0", 0, 128), QUAD8 if t > 1 else QUAD, A.is_equal)
+    ts(V("msk"), V("row0", 128, 192), CC, A.is_lt)
+
+    for k in (256, 448, 576):
+        fill("keep", k, k + 1, 0)
+    iota(V("small", 0, 20), [[-32, 10], [0, 2]], K)
+    fill("ini", 0, 96, 0)
+    for k in range(4):
+        iota(V("ini", 64 + 4 * k, 68 + 4 * k), [[384, 2], [768, 2]], 639 - 32 * k * (k + 1))
+    for k in START:
+        fill("ini", k, 32, START[k], 16)
+    fill("ini", 32 + KC, 64, 1, 16)
+    fill("ini", 32 + KD, 33 + KD, -1)
+    for base, table in ((512, ADDED), (1024, SUMMED)):
+        for kind, odd, line, w in table:
+            step = 16 << odd
+            mark(V("ct", base + 4 * (16 * odd + kind), base + 512, 4 * step), [[-step, 128 // step]], -16 * (odd + line), float(w))
+    fill("pj", 0, 16, 0)
+    for j, kind in enumerate((KF1, KRP, KRN, KD, KF2, KF3)):
+        iota(V("small", 32 + 2 * j, 34 + 2 * j), [[256, 2]], CX + kind)
+    iota(V("small", 44, 46), [[256, 2]], 0)
+    iota(V("small", 46, 48), [[KT - KC, 2]], KC)
+    iota(V("small", 48, 80), [[16, 32]], K)
+    iota(V("small", 80, 128), [[0, 3], [16, 16]], 0)
+    fill("rw", 0, 16, 0)
+    iota(V("rw", 176, 337), [[1, K + 1]], -K - 1)
+    fill("rw", 337, 497, 0)
+    for name, n in (("cr", K), ("c2", K), ("ur", C)):
+        fill(name, 0, 16, 0)
+        fill(name, 16 + n, T[name].shape[1], 0)
+    iota(V("thr"), [[1, K]], 80)
+
+    for lo in (0, K):
+        quant("qx", "sx", V("xin", 4 * lo, 4 * (lo + K)), lo, K)
 
     sent = 0
     for r in range(ROUNDS):
         partner = T.cores[rank ^ STEP[r]]
-        fill("rw", K, 2 * K, 200)
-        iota(V("ur", 16, 16 + C), [[1, C]], 0)
+        iota(V("ur", 16, 16 + C), [[1, C]], -240)
         mm(0, 128, "qu", "su", 0, "qx", "sx", 0)
-        mm(2, C, "qu2", "su2", 0, "qx", "sx", 0)
-        mm(1, C, "qu2", "su2", 0, "qx", "sx", 0)
-        mm(3, C, "qu2", "su2", 128, "qx", "sx", 0)
+        mm(6, 128, "qu2", "su2", 0, "qx", "sx", 0)
+        mm(7, 128, "qu2", "su2", 128, "qx", "sx", 0)
         mm(4, C - 128, "qu", "su", 0, "qx", "sx", 128)
+        mm(2, C, "qu2", "su2", 0, "qx", "sx", 0)
+        mm(3, C, "qu2", "su2", 128, "qx", "sx", 0)
+        mm(1, 224, "qu2", "su2", 0, "qx", "sx", 0)
+        mm(5, 224, "qu2", "su2", 128, "qx", "sx", 0)
         tr(V("ts", 0, 128), P(0, 128))
+        if r == 0:
+            quant("cq", "cs", V("ct", 0, 512), 512, 128)
 
-        def cmp_out(b, hh):
-            k = b // 2
-            return V("cmp", 4 * C * k + 2 * (b % 2) + hh, 4 * C * (k + 1), 4)
+        def slot(b, hh, lo=0, step=4):
+            c0 = 4 * TILE[b // 2]
+            return V("cmp", c0 + 4 * lo + 2 * hh + 1 - b % 2, c0 + 128 * (b + 1), step)
 
-        def s_cmp(b, hh):
-            s = V("ts", 32 * b + 16 * hh, 32 * b + 16 * hh + 1)
-            if b < 9:
-                act(cmp_out(b, hh), P(3 if hh else 2), ACT.Sign, bias=s, scale=-1.0)
-            else:
-                for lo in (0, K):
-                    act(V("cmp", 16 * C + 4 * lo + 3, 16 * C + 4 * lo + 4 * K, 4), V("ps3", lo, lo + K), ACT.Sign, bias=s, scale=-1.0)
-
-        def q_cmp(k):
-            for lo, n in (((0, C),) if k < 4 else ((0, K), (K, K))):
-                quant("cmq", "cms", V("cmp", 4 * (C * k + lo), 4 * (C * k + lo + n)), C * k + lo, n)
-            mm(0, C, "cq", "cs", 512, "cmq", "cms", C * k, start=k == 0, stop=k == 4, joint="rank%d" % r)
+        def sums(k, n, first=False, last=False):
+            mm(0, n, "cq", "cs", 512, "cmq", "cms", TILE[k], start=first, stop=last, joint="rank%d" % r)
 
         for step in ORDER.split():
-            kind, b = step[0], int(step[1])
-            if kind == "e":
-                s_cmp(b, 0)
-            elif kind == "o":
-                s_cmp(b, 1)
-            elif kind == "v":
-                ts(cmp_out(b, 0), P(1), V("ts", 32 * b, 32 * b + 1), A.is_lt, 2.0, A.mult)
+            kind = step[0]
+            b, hh = int((step + "00")[1]), int((step + "00")[2])
+            s = V("ts", 32 * b + 16 * hh, 32 * b + 16 * hh + 1)
+            if kind == "c":
+                ts(slot(b, hh), P((6, 7, 1, 5)[hh + 2 * (b > 3)], 32 * b + 32), s, A.is_lt)
+            elif kind == "s":
+                act(slot(b, hh), P(2 + hh, 32 * b + 32), ACT.Sign, bias=s, scale=-1.0)
+            elif kind == "r":
+                e = 2 * b + hh - 13
+                act(slot(b, hh), slot(b, hh), ACT.Relu, acc=V("acc", e, e + 1))
+            elif kind == "m":
+                tt(slot(b, 0, 32 * b, 2), slot(b, 0, 32 * b, 2), V("msk"), A.min)
+            elif kind == "n":
+                lo = 0 if b == 1 else 256
+                o = 256 + 384 * (1, 0, 3, 2)[b] - 256 + lo
+                scan(V("rs", o, o + 640 - lo), V("keep", lo, 640), V("cmp", 4 * (C + lo) + b, 3840, 4), 0.0, A.mult, A.add)
             elif kind == "q":
-                q_cmp(b)
+                n = 192 if b == 0 else 64 * (b + 1)
+                c0 = TILE[max(b, 1)]
+                quant("cmq", "cms", V("cmp", 4 * c0, 4 * (c0 + n)), c0, n)
+                if b == 0:
+                    sums(0, C, first=True)
+                    sums(1, 128)
+                else:
+                    sums(b, n, last=b == 3)
             elif kind == "t":
                 tr(V("ts", 128, C), P(4, C - 128))
-            else:
+            elif kind == "f":
                 for b in range(4):
                     mm(4 + b, C, "cq", "cs", 128 * b, "qx", "sx", 0)
-        if r == 0:
-            quant("cq", "cs", V("ct", 512, 1536), 640, 256)
+            else:
+                if r == 0:
+                    cp(V("ini", 80, 96), V("ini", 64, 80))
+                    tr(V("tab"), V("ini"))
+                    cp(V("le", 0, 1), V("tab", 64, 65))
+                    lin(V("ce"), V("small", 0, 20), 1.0, NEGC)
+                tt(V("em", 0, 256, 16), ind(V("rs"), V("le", 0, 1)), V("ce", 0, 16), A.add)
 
         def f_out(b):
             act(V("fw", 480 * b, 480 * b + C), P(4 + b))
 
-        BIG, ZERO = V("big"), V("st", 3, 4 * C, 4)
-        ZT, RHO, RR, CNT = V("col", 0, 1), V("col", 2, 3), V("col", 4, 5), V("col", 6, 7)
-        f_out(0)
-        for lo in (0, K):
-            ts(V("big", lo, lo + K), V("ps0", lo, lo + K), TH, A.is_lt, SH, A.subtract)
-        act(V("st", 2, 4 * C, 4), BIG, ACT.Identity, bias=SH, acc=CNT)
-        for lo in (0, K):
-            tt(V("wv", lo, lo + K), V("ps0", lo, lo + K), V("big", lo, lo + K), A.add)
-        f_out(1)
-        lin(RHO, CNT, -1.0 / 512, RB)
-        op("v", lambda: g.vector.tensor_reduce(T.col[:, 0:1], T.wv[:, 0:C], AxisListType.X, A.min), V("wv")[1], ZT[1])
-        ts(V("eqs"), V("wv"), ZT, A.is_equal, SGS, A.mult)
-        act(V("ne"), V("wv"), ACT.Sign, bias=ZT, scale=-1.0)
-        scan(V("pre"), V("eqs"), ZERO, INIT, A.add, A.add)
-        lin(RR, V("pre", C - 1, C), UP, RHO)
-        for lo in (0, K):
-            tt(V("yy", lo, lo + K), V("pre", lo, lo + K), V("ne", lo, lo + K), A.subtract)
-        for lo in (0, K):
-            ts(V("st", 4 * lo, 4 * (lo + K), 4), V("yy", lo, lo + K), RR, A.is_lt)
-        for lo in (0, K):
-            quant("stq", "sts", V("st", 4 * lo, 4 * (lo + K)), lo, K)
-        mm(2, C, "cq", "cs", 768, "stq", "sts", 0)
-        mm(1, C, "cq", "cs", 640, "stq", "sts", 0)
+        tt(V("em", 208, C, 16), V("acc", 0, 7), V("ce", 13, 20), A.add)
+        tr(V("et"), V("em"))
         if r == 0:
-            lin(V("na"), ZERO, 1.0, TA)
-            act(PAR, cf(5), ACT.Abs, bias=ODD, scale=-1.0)
-            lin(Q16, QQ, 16.0, 0.0)
-            lin(QN, QQ, -1.0 / 1024, 0.0)
-            lin(cf(21), ODD, -16.0, 32.0)
-            lin(V("tp", 0, 32), V("small", 64, 96), 1.0, QQ)
-            lin(C336, PAR, 336.0, Q16)
-            lin(C176, PAR, 176.0, Q16)
-            lin(cf(22), QQ, -1.0, cf(21))
-            lin(V("dw"), V("small", 32, 64), -1.0 / 1024, QN)
-            lin(BQ, C176, 1.0, cf(22))
-        f_out(2)
-        f_out(3)
+            quant("cq", "cs", V("ct", 512, 1536), 640, 256)
+            lin(V("na", 0, CX), V("e0", 0, CX), 0.0, NA)
+            lin(V("nb", 0, 1), INIT, 1.0, 0.0)
+            lin(V("rmp"), V("small", 48, 80), 1.0, QQ)
+        for lo in (0, K):
+            tt(V("cmp", 4 * lo, 4 * (lo + K), 4), V("ps0", lo, lo + K), V("et", lo, lo + K), A.is_lt)
+        for lo in (0, K):
+            quant("cmq", "cms", V("cmp", 4 * lo, 4 * (lo + K)), 640 + lo, K)
+        mm(2, CX, "cq", "cs", 768, "cmq", "cms", 640)
+        mm(1, CX, "cq", "cs", 640, "cmq", "cms", 640)
+        for b in range(4):
+            f_out(b)
         if r == 0:
-            ts(V("lj"), V("small", 0, 4), C336, A.add, 671.0, A.min)
-            ts(V("lk", 0, 1), ODD, 16.0, A.mult)
-            ts(V("lc", 0, 1), C176, 12.0, A.add, 351.0, A.min)
-            ts(V("ob", 48, 144), V("small", 96, 192), QQ, A.add)
+            ts(V("lj", 0, 12), V("small", 32, 44), CB, A.add, CX + C - 1.0, A.min)
+            ts(V("lj", 12, 14), V("small", 44, 46), C336, A.add, 671.0, A.min)
+            ts(V("lc", 0, 2), V("small", 46, 48), C176, A.add, 351.0, A.min)
+            ts(V("lc", 2, 3), CR, 16.0 + KT, A.add, 351.0, A.min)
+            ts(V("orr", 16, 64), V("small", 80, 128), QQ, A.add)
 
-        scan(V("nb"), P(2), V("na"), -160.0, A.add, A.add)
-        if r == 0:
-            ts(V("lbt", 0, 1), ODD, BQ, A.mult)
-            ts(V("lbt", 1, 3), V("small", 16, 18), BQ, A.add)
-        scan(V("pj", 17, 17 + C), P(1), V("nb"), -160.0, A.add, A.max)
-        if r == 0:
-            ts(V("lb", 0, 3), V("lbt", 0, 3), QQ, A.add, 383.0, A.min)
-        lin(V("pj", 368, 400), V("st", 3, 128, 4), 1.0, V("pj", 16 + C, 17 + C))
-        tr(V("tb", 0, C), V("pj", 16, 16 + C))
-        tr(V("tb", 672, 704), V("pj", 368, 400))
-        tr(V("tb", C, 672), V("pj", 0, 352))
-        tr2("tb", 704, "pj", 17, C)
-        lin(V("kap"), ind(V("tb", 672, 704), V("lk", 0, 1)), -1.0 / 1024, 2528.0 / 1024)
-        lin(V("nb1", 0, 32), ind(V("tb", 0, 672), V("lj", 0, 2)), 1025.0 / 1024, 1184.0 / 1024)
-        lin(V("nb1", 32, 64), ind(V("tb", 0, 672), V("lj", 2, 4)), 1025.0 / 1024, V("kap", 0, 1))
-        tt(V("nx"), ind(V("tb", 704, 1376), V("lj")), V("nb1"), A.subtract)
-        tt(V("ny", 0, 32), V("nx", 32, 64), V("nx", 0, 32), A.subtract)
-        tt(V("ny", 32, 64), V("nx", 0, 32), V("dw"), A.max)
-        tt(V("ny", 64, 96), V("ny", 0, 32), V("ny", 32, 64), A.max)
-        ts(V("osc1"), V("ny", 64, 96), -1024.0, A.mult)
+        scan(V("nb", 1, 1 + CX), P(2, CX), V("na"), INIT, A.add, A.add)
+        scan(V("pj", 16, 16 + CX), V("nb", 0, CX), P(1, CX), INIT, A.max, A.add)
+        tr(V("tb", CX, 2 * CX), V("pj", 16, 16 + CX))
+        tr(V("tb", 0, CX), V("pj", 0, CX))
+
+        def got(j, n=1):
+            return ind(V("tb", 0, CX + C), V("lj", 2 * j, 2 * (j + n)))
+
+        lin(V("l1", 32, 64), got(4), 1.0, V("tb", CX + C + 16 + KRP, CX + C + 17 + KRP))
+        cp(V("l1", 0, 32), got(3))
+        tt(V("l1", 64, 96), got(5), V("rmp"), A.min)
+        tt(V("l2", 0, 64), got(0, 2), V("l1", 0, 64), A.subtract)
+        tt(V("l2", 64, 96), got(2), V("l1", 64, 96), A.add)
+        tt(V("l3", 0, 32), V("l2", 0, 32), V("l2", 32, 64), A.max)
+        tt(V("l3", 32, 64), V("l3", 0, 32), V("l2", 64, 96), A.min)
+        ts(V("osc1"), V("l3", 32, 64), 256.0, A.add)
         scatter(V("rw"), V("osc1", 0, 20), V("pj", 16, 16 + C))
-        tt(V("pr", 16, 16 + K), V("rw", 0, K), V("rw", K, 2 * K), A.min)
-        tr2("tp", 32, "pr", 16, K)
-        ts(V("ob", 0, 48), ind(V("tp"), V("lb", 0, 3)), 160.0, A.add)
-        for src, up, tall in ((0, 1, 1), (1, 1, 1), (2, 1, 1), (0, 3, 1), (0, 2, 2)):
-            cp(V("ob", 16 + 32 * up, 48 + 32 * up, quad=src + up, tall=tall), V("ob", 16, 48, quad=src, tall=tall))
+        tr2("tp", "rw", K)
+        ts(V("ob"), ind(V("tp"), V("lc", 0, 2)), 160.0, A.add)
 
-        def both(dst, d0, src, lst, c0, n):
-            act(V(dst, d0, d0 + 16 * n), ind(src, V(lst, c0, c0 + n)))
-            cp(V(dst, d0 + 16 * n, d0 + K), ind(src, V(lst, c0 + n, c0 + 10)))
+        def z_part(name, b, lst, e):
+            e(V(name, b, 4 * K, 4), ind(V("fw", 480 * b, 480 * b + C), lst))
 
-        act(V("ca"), ind(V("rw", 0, K), V("ob", 0, 10)))
-        both("cb", 0, V("ca"), "ob", 64, 6)
-        both("la", 0, V("idr"), "ob", 128, 4)
-        both("ca", 0, V("cb"), "ob", 48, 6)
-        both("lr", 16, V("la"), "ob", 112, 4)
-        both("cb", 0, V("ca"), "ob", 96, 6)
-        tr2("tl", 0, "lr", 16, K)
-        both("ca", 0, V("cb"), "ob", 80, 6)
-        ts(V("oll"), ind(V("tl"), V("lc", 0, 1)), 0.0, A.add)
-        both("cr", 16, V("ca"), "oll", 0, 4)
-        tr2("tc", 0, "cr", 16, K)
-        ts(V("ocl"), ind(V("tc"), V("lc", 0, 1)), 160.0, A.add)
-        PL = V("ocl", 0, 10)
+        def hand(stage, src, up, tall=1):
+            cp(V("orr", 16 * stage, 16 * stage + 10, quad=src + up, tall=tall), V("orr", 0, 10, quad=src, tall=tall))
+
+        L1 = V("ob", 0, 10)
+        act(V("cr", 16, 16 + K), ind(V("rw", 176, 497), V("ob", 16, 26)))
+        z_part("z", 0, L1, cp)
+        z_part("z", 2, L1, act)
+        tr2("tc", "cr", K)
+        z_part("z", 1, L1, cp)
+        z_part("z", 3, L1, act)
+        ts(V("orr", 0, 16), ind(V("tc"), V("lc", 2, 3)), 160.0, A.add)
+        hand(1, 2, 1)
+        hand(1, 1, 1)
+        quant("qa", "sa", V("z"))
+        hand(2, 0, 2, 2)
+        pick("b", "a", V("orr", 16, 26))
+        hand(3, 0, 3)
+        hand(3, 0, 1)
+        pick("c", "b", V("orr", 32, 42))
+        pick("d", "c", V("orr", 48, 58))
+
+        def both(dst, d0, src, lst, n):
+            act(V(dst, d0, d0 + 16 * n), ind(src, V("orr", lst, lst + n)))
+            cp(V(dst, d0 + 16 * n, d0 + K), ind(src, V("orr", lst + n, lst + 10)))
 
         for b in range(4):
-            (cp if b < 2 else act)(V("z", b, 4 * K, 4), ind(V("fw", 480 * b, 480 * b + C), PL))
-        quant("qz", "sz", V("z"))
-        for b in range(4):
-            mm(4 + b, K, "qw", "sw", 128 * b, "qz", "sz", 0)
+            mm(4 + b, K, "qw", "sw", 128 * b, "qd", "sd", 0)
+        both("ca", 0, V("rw", 16, 16 + K), 16, 4)
         for b in range(4):
             if b % 2:
                 ts(V("h", b, 4 * K, 4), P(4 + b, K), 0.0, A.max, 0.015625, A.mult)
@@ -474,12 +497,20 @@ def rank_program(g, core, T, topo):
         op("g", send, regs(V("outq%d" % r), V("outs%d" % r)), [])
         sent += sum(popcount(p[4]) for p in pieces)
 
+        both("cb", 0, V("ca"), 32, 4)
+        both("c2", 16, V("cb"), 48, 4)
+        tr2("td", "c2", K)
+        ts(V("ocl"), ind(V("td"), V("lc", 0, 1)), 160.0, A.add)
+        PL = V("ocl", 0, 10)
+        for b in range(3):
+            z_part("z2", b, PL, act)
         scatter(V("ur", 16, 16 + C), PL, V("thr"))
-        tr2("tu", 0, "ur", 16, C)
-        cp(V("ou"), ind(V("tu"), V("lj", 2, 4)))
+        tr2("tu", "ur", C)
+        ts(V("ou"), ind(V("tu"), V("lj", 12, 14)), 240.0, A.add)
+        z_part("z2", 3, PL, cp)
         if r == ROUNDS - 1:
-            lin(V("plb"), V("cr", 16, 16 + K), 1.0, 160.0)
-            dma("y", T.pl[:], T.plb[12:128:16, :], V("plb")[1], [], must=True)
+            lin(V("plb"), V("c2", 16, 16 + K), 1.0, 160.0)
+            dma("y", T.pl[:], T.plb[KC:128:16, :], V("plb")[1], [], must=True)
         if r == 0:
             quant("qv", "sv", V("vin"))
 
@@ -487,7 +518,7 @@ def rank_program(g, core, T, topo):
         for b in range(4):
             mm(4 + b, K, "cq", "cs", 128 * b, "landq%d" % r, "lands%d" % r, 0, ext=[(T.sem["arr%d" % r], arrive)] if b == 0 else ())
         for b in range(4):
-            tt(V("fw", 480 * b + C, 480 * b + 480), P(4 + b, K), V("z", b, 4 * K, 4), A.add)
+            tt(V("fw", 480 * b + C, 480 * b + 480), P(4 + b, K), V("z2", b, 4 * K, 4), A.add)
         for e, b, hf in UPDATE:
             if b < 4:
                 (cp if e == "v" else act)(V("xn", 2 * C * hf + b, 2 * C * (hf + 1), 4), ind(V("fw", 480 * b, 480 * b + 480), V("ou", 10 * hf, 10 * hf + 10)))

@@ -4,17 +4,18 @@ from concourse.mybir import dt, AluOpType, ActivationFunctionType
 C, K, ROUNDS = 320, 160, 3
 STEP = [1, 2, 4]
 BIG = 1024
+LO = 352
 CX = C + 32
 X4, U8, U16, BF, F32, I32 = "float8_e4m3fn_x4", "uint8", "uint16", "bfloat16", "float32", "int32"
 SIZES = {
-    BF: {"xin": 4 * C, "uin": 512, "vin": 512, "e0": 520, "ct": 1536, "row0": 192, "msk": 64, "keep": 640, "cmp": 3840,
-         "rs": 1792, "em": C, "et": C, "na": CX, "nb": CX + 4, "pj": 384, "tb": 2 * CX, "rw": 992, "tp": 352,
+    BF: {"xin": 4 * C, "uin": 512, "vin": 512, "e0": 520, "ct": 1536, "row0": 448, "msk": C, "keep": 704, "cmp": 3840,
+         "dg": 2 * C, "rd": 2 * C, "rs": 1536, "em": C, "et": C, "na": CX, "nb": CX + 4, "pj": 384, "tb": 2 * CX, "rw": 832, "tp": 352,
          "cr": 192, "tc": 352, "ca": K, "cb": K, "c2": 192, "td": 352, "ur": 352, "tu": 672, "thr": K,
          "fw": 4 * 480, "z": 4 * K, "z2": 4 * K, "h": 4 * K, "xn": 4 * C},
-    F32: {"cf": 16, "small": 128, "ini": 96, "tab": 96, "ts": C, "acc": 8, "ce": 20, "rmp": 32,
-          "l1": 96, "l2": 96, "l3": 64, "plb": K, "yb": C},
+    F32: {"cf": 16, "small": 144, "ini": 160, "tab": 160, "ts": 2 * C, "acc": 8, "ce": 32, "cd": 32, "cst": 48,
+          "l1": 80, "l2": 128, "l3": 80, "plb": K, "yb": C},
     I32: {"ci": 8, "lui": 16},
-    U16: {"lu": 16, "lj": 16, "lc": 4, "le": 2, "osc1": 32, "ob": 32, "orr": 64, "ocl": 16, "ou": 32},
+    U16: {"lu": 16, "lj": 16, "lc": 4, "le": 4, "osc1": 32, "ob": 32, "orr": 64, "rev": 10, "ocl": 16, "ou": 32},
     X4: {"qx": C, "qu": 128, "qu2": 256, "qv": 128, "qw": 512, "cq": 896, "cmq": 1216, "qa": K, "qb": K, "qc": K, "qd": K},
     U8: {"sx": C, "su": 128, "su2": 256, "sv": 128, "sw": 512, "cs": 896, "cms": 1216, "sa": K, "sb": K, "sc": K, "sd": K},
 }
@@ -32,13 +33,14 @@ SEMAPHORES += ["hop%d" % r for r in range(ROUNDS)] + ["arr%d" % r for r in range
 
 A = AluOpType
 ACT = ActivationFunctionType
-KT, KC, KF1, KF2, KF3, KRP, KRN, KD = range(8)
+KT, KC, KRP, KD, KRN, KZ, KF1, KF2, KF3 = range(9)
 ADDED = ((KT, 0, 0, 1), (KD, 0, 0, -1), (KF1, 0, 0, -BIG), (KF2, 1, -1, BIG), (KF2, 1, 0, -BIG), (KF3, 1, 0, BIG), (KF3, 1, 1, -BIG))
 SUMMED = ((KT, 1, 1, 1), (KRN, 1, 1, 1), (KRN, 1, 0, -1), (KRP, 1, 0, 1), (KRP, 1, -1, -1), (KD, 1, -1, -1))
-START = {KT: -K, KC: -K, KF1: BIG, KF2: BIG + 80, KF3: BIG, KRN: 81, KD: 241}
+START = {KT: -K, KC: -K, KF1: BIG, KF2: BIG, KF3: BIG, KD: K + 1}
 TILE = [896, 768, 576, 320, 0]
-ORDER = ("c00 c01 c10 c11 t s90 s91 c20 c21 m0 m1 c30 c31 s80 s81 m9 m2 c40 c41 m3 r90 m8 r91 q0 c50 c51 m4 r80 r81 c60 f m5 s70 s71 s61 q2 q4 "
-         "n0 m7 m6 r70 r71 n2 n3 r61 n1 e q3")
+ORDER = ("t00 t01 c10 t10 s90 c20 c11 c21 t11 s91 s80 s81 s70 s71 d00 d11 d01 d10 c30 c31 c40 c41 c50 q0 c51 m0 m1 c60 c61 f "
+         "r90 r91 r80 r81 r70 r71 r61 k0 q4 k1 n2 n0 g n1 n3 q3 e q2")
+LAST = "q2"
 UPDATE = (("s", 0, 0), ("s", 1, 0), ("v", 2, 0), ("v", 3, 0), ("s", 0, 1), ("s", 1, 1), ("v", 3, 1), ("v", 4, 0), ("s", 2, 1), ("v", 4, 1))
 
 
@@ -199,9 +201,9 @@ def rank_program(g, core, T, topo):
     def tr(out, a):
         op("v", lambda: g.vector.transpose(out[0], a[0]), a[1], out[1])
 
-    def tr2(out, row, n):
-        tr(V(out, 0, n), V(row, 16, 16 + n))
-        tr(V(out, n, 2 * n + 32), V(row, 0, n + 32))
+    def tr2(out, row, n, r0=16):
+        tr(V(out, 0, n), V(row, r0, r0 + n))
+        tr(V(out, n, 2 * n + 32), V(row, r0 - 16, r0 + n + 16))
 
     def scan(out, d0, d1, init, o0, o1):
         op("v", lambda: g.vector.tensor_tensor_scan(out[0], d0[0], d1[0], val(init), o0, o1), regs(d0, d1, init), out[1])
@@ -258,104 +260,106 @@ def rank_program(g, core, T, topo):
         return V("ci", k, k + 1)
 
     dma("s", T.uin[:], T.u[:], [], V("uin")[1])
-    dma("y", T.xin[:], T.x[:], [], V("xin")[1])
+    for lo in (0, 2 * C):
+        dma("y", T.xin[:, lo:lo + 2 * C], T.x[:, lo:lo + 2 * C], [], V("xin", lo, lo + 2 * C)[1])
     dma("y", T.qw[:].bitcast(dt.uint8), T.wc[:], V("xin")[1], V("qw")[1])
     dma("y", T.sw[:], T.ws[:], [], V("sw")[1])
     dma("y", T.vin[:], T.v[:], [], V("vin")[1])
 
-    QUAD, QUAD8, CC, QQ, ODD, BIT, PAR, Q16, NEGC, CB, C336, C176, CR = [cf(k) for k in range(13)]
+    QUAD, CC, QQ, ODD, BIT, PAR, Q16, C304, CB, C336, C176, CR = [cf(k) for k in range(1, 13)]
     INIT, NA = V("tab", 0, 1), V("tab", 32, 33)
+    ms(V("em"), 0.0)
     ms(V("e0"), 0.0)
-    ms(V("ct", 512, 1536), 0.0)
+    ms(V("ini"), 0.0)
     iota(ci(0), [[0, 1]], 0, 1, whole=True)
     iota(V("lui"), [[16, 2], [32, 4], [0, 2]], 0, whole=True)
     mark(V("e0", 4, 516, 4), [[-1, 128]], 0, 1.0)
     iota(V("row0", 0, 128), [[1, 4], [8, 2], [0, 16]], 0)
-    iota(V("row0", 128, 192), [[1, 32], [0, 2]], 0)
-    quant("cmq", "cms", V("ct", 512, 1536), 960, 256)
+    iota(V("row0", 128, 128 + C), [[0, 10], [1, 32]], 0)
+    for k in range(4):
+        lin(V("ct", 512 + 256 * k, 768 + 256 * k), V("em", 0, 256), 0.0, 0.0)
+    for k in range(2):
+        lin(V("keep", 192 * k, 192 * (k + 1)), V("em", 0, 192), 0.0, 1.0)
+    iota(V("small", 0, 32), [[-32, 16], [0, 2]], K - 31)
     for k in range(5):
-        fill("cmp", 4 * (TILE[k] + 64 * k + 32) + 1, 4 * (TILE[k] + 64 * k + 64), 0, 2)
+        fill("cmp", 4 * (TILE[k] + 64 * k + 32) + (k < 4), 4 * (TILE[k] + 64 * k + 64), 0, 2)
     ts(ci(1), ci(0), 5, A.arith_shift_right)
     ts(ci(2), ci(0), 31, A.bitwise_and)
     ts(ci(3), ci(0), 15, A.bitwise_and)
     ts(ci(4), ci(0), 4, A.arith_shift_right, 1, A.bitwise_and)
     ts(ci(5), ci(0), 1, A.bitwise_and)
     cp(V("lu"), V("lui"))
-    cp(QUAD, ci(1))
-    cp(V("cf", 2, 6), V("ci", 2, 6))
-    lin(QUAD8, QUAD, 1.0, 8.0)
-    lin(NEGC, CC, -1.0, 0.0)
+    cp(V("cf", 1, 6), V("ci", 1, 6))
+    for b in range(4):
+        quant("cq", "cs", V("e0", 4 - b, 516 - b), 128 * b, 128)
+    for t in range(4):
+        ts(V("ct", t, 512, 4), V("row0", 0, 128), -8.0 * (t // 2), A.add, QUAD, A.is_equal)
+    quant("qu", "su", V("uin"))
+    quant("cmq", "cms", V("ct", 512, 1024), 960, 128)
+    op("v", lambda: g.vector.tensor_copy(T.qu2[:, 0:256].bitcast(dt.uint32), T.qu[:, 0:128].bitcast(dt.uint32).indirect(T.lu[:, 0:16])),
+       regs(V("qu"), V("lu")), V("qu2")[1])
+    act(V("su2"), ind(V("su"), V("lu")))
+    for lo in (0, K):
+        quant("qx", "sx", V("xin", 4 * lo, 4 * (lo + K)), lo, K)
+    quant("cmq", "cms", V("ct", 1024, 1536), 1088, 128)
+    quant("cq", "cs", V("ct", 0, 512), 512, 128)
+    ts(V("msk"), V("row0", 128, 128 + C), CC, A.is_lt, -1.0, A.mult)
+    act(V("keep", 384, 384 + C), V("row0", 128, 128 + C), ACT.Sign)
+    lin(V("rs", 1152, 1344), V("em", 0, 192), 0.0, 0.0)
+    lin(V("ce"), V("small", 0, 32), 1.0, CC)
     act(PAR, BIT, ACT.Abs, bias=ODD, scale=-1.0)
     lin(Q16, QQ, 16.0, 0.0)
+    lin(C304, BIT, 304.0, Q16)
     lin(CB, PAR, 16.0 - CX, Q16)
     lin(C336, PAR, 336.0, Q16)
     lin(C176, PAR, 176.0, Q16)
     lin(CR, ODD, -16.0, C176)
-    lin(V("em"), V("e0", 0, C), 0.0, 0.0)
-    lin(V("keep", 0, C), V("e0", 0, C), 0.0, 1.0)
-    lin(V("keep", C, 2 * C), V("e0", 0, C), 0.0, 1.0)
 
-    quant("qu", "su", V("uin"))
-    op("v", lambda: g.vector.tensor_copy(T.qu2[:, 0:256].bitcast(dt.uint32), T.qu[:, 0:128].bitcast(dt.uint32).indirect(T.lu[:, 0:16])),
-       regs(V("qu"), V("lu")), V("qu2")[1])
-    act(V("su2"), ind(V("su"), V("lu")))
-    for b in range(4):
-        quant("cq", "cs", V("e0", 4 - b, 516 - b), 128 * b, 128)
-    for t in range(4):
-        ts(V("ct", t, 512, 4), V("row0", 0, 128), QUAD8 if t > 1 else QUAD, A.is_equal)
-    ts(V("msk"), V("row0", 128, 192), CC, A.is_lt)
-
-    for k in (256, 448, 576):
-        fill("keep", k, k + 1, 0)
-    iota(V("small", 0, 20), [[-32, 10], [0, 2]], K)
-    fill("ini", 0, 96, 0)
-    for k in range(4):
-        iota(V("ini", 64 + 4 * k, 68 + 4 * k), [[384, 2], [768, 2]], 639 - 32 * k * (k + 1))
+    fill("keep", 192, 384, 0, 128)
+    iota(V("small", 128, 130), [[256, 2]], 31)
+    fill("ini", 64, 80, 1152)
+    for k in range(3):
+        iota(V("ini", 66 + 4 * k, 70 + 4 * k), [[384, 2], [768, 2]], 383 - 32 * k * (k + 1))
     for k in START:
         fill("ini", k, 32, START[k], 16)
+    fill("ini", KRP, KRP + 1, BIG)
     fill("ini", 32 + KC, 64, 1, 16)
     fill("ini", 32 + KD, 33 + KD, -1)
     for base, table in ((512, ADDED), (1024, SUMMED)):
         for kind, odd, line, w in table:
             step = 16 << odd
-            mark(V("ct", base + 4 * (16 * odd + kind), base + 512, 4 * step), [[-step, 128 // step]], -16 * (odd + line), float(w))
+            mark(V("ct", base + 4 * (16 * odd + kind) + 1, base + 512, 4 * step), [[-step, 128 // step]], -16 * (odd + line), float(w))
     fill("pj", 0, 16, 0)
-    for j, kind in enumerate((KF1, KRP, KRN, KD, KF2, KF3)):
-        iota(V("small", 32 + 2 * j, 34 + 2 * j), [[256, 2]], CX + kind)
+    for odd, first, turn in ((0, CX, 32 - CX), (1, 16, CX)):
+        iota(V("ini", 96 + 16 * odd, 112 + 16 * odd), [[32, 2], [turn, 2], [1, 4]], first + KZ)
+        iota(V("ini", 128 + 16 * odd, 144 + 16 * odd), [[32, 4], [turn, 2], [1, 2]], first + KD)
+    iota(V("small", 32, 38), [[64, 6]], 0)
+    iota(V("small", 38, 42), [[128, 4]], 0)
+    iota(V("small", 42, 44), [[256, 2]], CX + KRP)
     iota(V("small", 44, 46), [[256, 2]], 0)
+    iota(V("small", 48, 80), [[16, 32]], K + 1)
+    iota(V("cst"), [[0, 24], [K + 2 - LO, 2]], 0)
     iota(V("small", 46, 48), [[KT - KC, 2]], KC)
-    iota(V("small", 48, 80), [[16, 32]], K)
     iota(V("small", 80, 128), [[0, 3], [16, 16]], 0)
-    fill("rw", 0, 16, 0)
-    iota(V("rw", 176, 337), [[1, K + 1]], -K - 1)
-    fill("rw", 337, 497, 0)
+    iota(V("rw", 0, K + 1), [[1, K + 1]], -K - 1)
+    fill("rw", K + 1, LO, 0)
+    fill("rw", LO + K, LO + K + 16, 0)
     for name, n in (("cr", K), ("c2", K), ("ur", C)):
         fill(name, 0, 16, 0)
         fill(name, 16 + n, T[name].shape[1], 0)
     iota(V("thr"), [[1, K]], 80)
-
-    for lo in (0, K):
-        quant("qx", "sx", V("xin", 4 * lo, 4 * (lo + K)), lo, K)
+    iota(V("small", 132, 142), [[-16, 10]], K - 1)
 
     sent = 0
     for r in range(ROUNDS):
         partner = T.cores[rank ^ STEP[r]]
         iota(V("ur", 16, 16 + C), [[1, C]], -240)
-        mm(0, 128, "qu", "su", 0, "qx", "sx", 0)
-        mm(6, 128, "qu2", "su2", 0, "qx", "sx", 0)
-        mm(7, 128, "qu2", "su2", 128, "qx", "sx", 0)
-        mm(4, C - 128, "qu", "su", 0, "qx", "sx", 128)
-        mm(2, C, "qu2", "su2", 0, "qx", "sx", 0)
-        mm(3, C, "qu2", "su2", 128, "qx", "sx", 0)
-        mm(1, 224, "qu2", "su2", 0, "qx", "sx", 0)
-        mm(5, 224, "qu2", "su2", 128, "qx", "sx", 0)
-        tr(V("ts", 0, 128), P(0, 128))
-        if r == 0:
-            quant("cq", "cs", V("ct", 0, 512), 512, 128)
+        for bank, hh, lo, n in ((6, 0, 0, K), (7, 1, 0, K), (4, 0, K, K), (2, 0, 0, 288), (0, 1, K, K), (3, 1, 0, 288), (1, 0, 0, 192), (5, 1, 0, 192)):
+            mm(bank, n, "qu2", "su2", 128 * hh, "qx", "sx", lo)
 
-        def slot(b, hh, lo=0, step=4):
-            c0 = 4 * TILE[b // 2]
-            return V("cmp", c0 + 4 * lo + 2 * hh + 1 - b % 2, c0 + 128 * (b + 1), step)
+        def slot(b, hh):
+            c0 = 4 * TILE[(b - 1) // 2]
+            return V("cmp", c0 + 2 * hh + (b % 2 if b < 9 else 0), c0 + 128 * b, 4)
 
         def sums(k, n, first=False, last=False):
             mm(0, n, "cq", "cs", 512, "cmq", "cms", TILE[k], start=first, stop=last, joint="rank%d" % r)
@@ -363,20 +367,28 @@ def rank_program(g, core, T, topo):
         for step in ORDER.split():
             kind = step[0]
             b, hh = int((step + "00")[1]), int((step + "00")[2])
-            s = V("ts", 32 * b + 16 * hh, 32 * b + 16 * hh + 1)
+            s = V("ts", C * hh + 32 * b, C * hh + 32 * b + 1)
             if kind == "c":
-                ts(slot(b, hh), P((6, 7, 1, 5)[hh + 2 * (b > 3)], 32 * b + 32), s, A.is_lt)
+                ts(slot(b, hh), P(1 + 4 * hh if b == 6 else 6 + hh, 32 * b), s, A.is_lt)
             elif kind == "s":
-                act(slot(b, hh), P(2 + hh, 32 * b + 32), ACT.Sign, bias=s, scale=-1.0)
+                act(slot(b, hh), P(2 + hh, 32 * b), ACT.Sign, bias=s, scale=-1.0)
             elif kind == "r":
                 e = 2 * b + hh - 13
                 act(slot(b, hh), slot(b, hh), ACT.Relu, acc=V("acc", e, e + 1))
+            elif kind in "td":
+                bank, o = P((6, 7, 4, 0)[2 * b + hh], K), C * hh + K * b
+                if kind == "t":
+                    tr(V("ts", o, o + K), bank)
+                else:
+                    tt(V("dg", o, o + K), bank, V("ts", o, o + K), A.is_ge)
             elif kind == "m":
-                tt(slot(b, 0, 32 * b, 2), slot(b, 0, 32 * b, 2), V("msk"), A.min)
+                scan(V("cmp", 2 * b + 1, 4 * C, 4), V("dg", C * b, C * (b + 1)), V("msk"), 0.0, A.max, A.mult)
+            elif kind == "k":
+                scan(V("rd", C * b, C * (b + 1)), V("keep", 384, 384 + C), V("cmp", 2 * b + 1, 4 * C, 4), 0.0, A.mult, A.add)
             elif kind == "n":
-                lo = 0 if b == 1 else 256
-                o = 256 + 384 * (1, 0, 3, 2)[b] - 256 + lo
-                scan(V("rs", o, o + 640 - lo), V("keep", lo, 640), V("cmp", 4 * (C + lo) + b, 3840, 4), 0.0, A.mult, A.add)
+                lo = 192 if b == 2 else 0
+                o = 384 * (1, 0, 3, 2)[b]
+                scan(V("rs", o + lo, o + 384), V("keep", lo, 384), V("cmp", 4 * (TILE[2] + lo) + b, 3840, 4), 0.0, A.mult, A.add)
             elif kind == "q":
                 n = 192 if b == 0 else 64 * (b + 1)
                 c0 = TILE[max(b, 1)]
@@ -385,63 +397,79 @@ def rank_program(g, core, T, topo):
                     sums(0, C, first=True)
                     sums(1, 128)
                 else:
-                    sums(b, n, last=b == 3)
-            elif kind == "t":
-                tr(V("ts", 128, C), P(4, C - 128))
+                    sums(b, n, last=step == LAST)
             elif kind == "f":
                 for b in range(4):
                     mm(4 + b, C, "cq", "cs", 128 * b, "qx", "sx", 0)
+            elif kind == "g":
+                tt(V("cd"), ind(V("rd"), V("le", 2, 4)), V("ce"), A.add)
             else:
-                if r == 0:
-                    cp(V("ini", 80, 96), V("ini", 64, 80))
-                    tr(V("tab"), V("ini"))
-                    cp(V("le", 0, 1), V("tab", 64, 65))
-                    lin(V("ce"), V("small", 0, 20), 1.0, NEGC)
-                tt(V("em", 0, 256, 16), ind(V("rs"), V("le", 0, 1)), V("ce", 0, 16), A.add)
+                tt(V("em", 0, 256, 16), ind(V("rs"), V("le", 0, 1)), V("cd", 0, 16), A.add)
+            if r == 0 and step == "q0":
+                cp(V("ini", 80, 96), V("ini", 64, 80))
+            if r == 0 and step == "k0":
+                tr(V("tab", 0, 96), V("ini", 0, 96))
+                ts(V("le", 2, 4), V("small", 128, 130), C304, A.add, 2.0 * C - 1, A.min)
+            if r == 0 and step == "k1":
+                cp(V("le", 0, 1), V("tab", 64, 65))
 
         def f_out(b):
             act(V("fw", 480 * b, 480 * b + C), P(4 + b))
 
-        tt(V("em", 208, C, 16), V("acc", 0, 7), V("ce", 13, 20), A.add)
+        tt(V("em", 208, C, 16), V("acc", 0, 7), V("cd", 13, 20), A.add)
         tr(V("et"), V("em"))
         if r == 0:
-            quant("cq", "cs", V("ct", 512, 1536), 640, 256)
+            quant("cq", "cs", V("ct", 1024, 1536), 768, 128)
             lin(V("na", 0, CX), V("e0", 0, CX), 0.0, NA)
             lin(V("nb", 0, 1), INIT, 1.0, 0.0)
-            lin(V("rmp"), V("small", 48, 80), 1.0, QQ)
+        HALVES = ((0, K, 2, 1), (K, CX, 3, 0))
         for lo in (0, K):
-            tt(V("cmp", 4 * lo, 4 * (lo + K), 4), V("ps0", lo, lo + K), V("et", lo, lo + K), A.is_lt)
-        for lo in (0, K):
+            tt(V("cmp", 4 * lo + 1, 4 * (lo + K), 4), V("ps0", lo, lo + K), V("et", lo, lo + K), A.is_lt)
+        for lo, hi, b2, b1 in HALVES:
             quant("cmq", "cms", V("cmp", 4 * lo, 4 * (lo + K)), 640 + lo, K)
-        mm(2, CX, "cq", "cs", 768, "cmq", "cms", 640)
-        mm(1, CX, "cq", "cs", 640, "cmq", "cms", 640)
+            mm(b2, hi - lo, "cq", "cs", 768, "cmq", "cms", 640 + lo)
+            if r == 0 and lo == 0:
+                quant("cq", "cs", V("ct", 512, 1024), 640, 128)
+            mm(b1, hi - lo, "cq", "cs", 640, "cmq", "cms", 640 + lo)
         for b in range(4):
             f_out(b)
         if r == 0:
-            ts(V("lj", 0, 12), V("small", 32, 44), CB, A.add, CX + C - 1.0, A.min)
-            ts(V("lj", 12, 14), V("small", 44, 46), C336, A.add, 671.0, A.min)
+            lin(V("l2", 0, 128, 4), V("small", 48, 80), 1.0, QQ)
+            tr(V("tab", 96, 160), V("ini", 96, 160))
+            ts(V("lj", 10, 12), V("small", 42, 44), CB, A.add, CX + C - 1.0, A.min)
+
+        for lo, hi, b2, b1 in HALVES:
+            scan(V("nb", 1 + lo, 1 + hi), P(b2, hi - lo), V("na", lo, hi), V("nb", lo, lo + 1), A.add, A.add)
+            if lo:
+                tr(V("tb", 0, K), V("pj", 0, K))
+            elif r == 0:
+                ts(V("lj", 0, 6), V("small", 32, 38), V("tab", 96, 97), A.add, CX + C - 1.0, A.min)
+            scan(V("pj", 16 + lo, 16 + hi), V("nb", lo, hi), P(b1, hi - lo), V("pj", 15 + lo, 16 + lo) if lo else INIT, A.max, A.add)
+        tr(V("tb", CX, CX + K), V("pj", 16, 16 + K))
+        if r == 0:
+            ts(V("lj", 6, 10), V("small", 38, 42), V("tab", 128, 129), A.add, CX + C - 1.0, A.min)
+        tr(V("tb", CX + K, 2 * CX), V("pj", 16 + K, 16 + CX))
+        tr(V("tb", K, CX), V("pj", K, CX))
+
+        def got(lo, hi):
+            return ind(V("tb", 0, CX + C), V("lj", lo, hi))
+
+        lin(V("l2", 2, 128, 4), got(10, 12), -1.0, V("tb", CX + C + 16 + KRP, CX + C + 17 + KRP))
+        tt(V("l2", 1, 96, 2), got(6, 9), V("cst"), A.add)
+        lin(V("l1", 0, 32), got(0, 2), 1.0, -400.0)
+        ts(V("l1", 32, 80), got(2, 5), -400.0, A.add)
+        if r == 0:
             ts(V("lc", 0, 2), V("small", 46, 48), C176, A.add, 351.0, A.min)
+        scan(V("l3"), V("l1"), V("l2", 0, 80), 0.0, A.min, A.max)
+        if r == 0:
             ts(V("lc", 2, 3), CR, 16.0 + KT, A.add, 351.0, A.min)
+        ts(V("osc1", 0, 20), V("l3", 3, 80, 4), LO - 1.0, A.add)
+        if r == 0:
             ts(V("orr", 16, 64), V("small", 80, 128), QQ, A.add)
-
-        scan(V("nb", 1, 1 + CX), P(2, CX), V("na"), INIT, A.add, A.add)
-        scan(V("pj", 16, 16 + CX), V("nb", 0, CX), P(1, CX), INIT, A.max, A.add)
-        tr(V("tb", CX, 2 * CX), V("pj", 16, 16 + CX))
-        tr(V("tb", 0, CX), V("pj", 0, CX))
-
-        def got(j, n=1):
-            return ind(V("tb", 0, CX + C), V("lj", 2 * j, 2 * (j + n)))
-
-        lin(V("l1", 32, 64), got(4), 1.0, V("tb", CX + C + 16 + KRP, CX + C + 17 + KRP))
-        cp(V("l1", 0, 32), got(3))
-        tt(V("l1", 64, 96), got(5), V("rmp"), A.min)
-        tt(V("l2", 0, 64), got(0, 2), V("l1", 0, 64), A.subtract)
-        tt(V("l2", 64, 96), got(2), V("l1", 64, 96), A.add)
-        tt(V("l3", 0, 32), V("l2", 0, 32), V("l2", 32, 64), A.max)
-        tt(V("l3", 32, 64), V("l3", 0, 32), V("l2", 64, 96), A.min)
-        ts(V("osc1"), V("l3", 32, 64), 256.0, A.add)
         scatter(V("rw"), V("osc1", 0, 20), V("pj", 16, 16 + C))
-        tr2("tp", "rw", K)
+        tr2("tp", "rw", K, LO)
+        if r == 0:
+            ts(V("lj", 12, 14), V("small", 44, 46), C336, A.add, 671.0, A.min)
         ts(V("ob"), ind(V("tp"), V("lc", 0, 2)), 160.0, A.add)
 
         def z_part(name, b, lst, e):
@@ -451,16 +479,16 @@ def rank_program(g, core, T, topo):
             cp(V("orr", 16 * stage, 16 * stage + 10, quad=src + up, tall=tall), V("orr", 0, 10, quad=src, tall=tall))
 
         L1 = V("ob", 0, 10)
-        act(V("cr", 16, 16 + K), ind(V("rw", 176, 497), V("ob", 16, 26)))
+        act(V("cr", 16, 16 + K), ind(V("rw", 0, LO - 16), V("ob", 16, 26)))
         z_part("z", 0, L1, cp)
         z_part("z", 2, L1, act)
-        tr2("tc", "cr", K)
         z_part("z", 1, L1, cp)
+        tr2("tc", "cr", K)
         z_part("z", 3, L1, act)
-        ts(V("orr", 0, 16), ind(V("tc"), V("lc", 2, 3)), 160.0, A.add)
+        ts(V("orr", 0, 16), ind(V("tc"), V("lc", 2, 3)), -1.0, A.mult, -1.0, A.add)
+        quant("qa", "sa", V("z"))
         hand(1, 2, 1)
         hand(1, 1, 1)
-        quant("qa", "sa", V("z"))
         hand(2, 0, 2, 2)
         pick("b", "a", V("orr", 16, 26))
         hand(3, 0, 3)
@@ -474,7 +502,7 @@ def rank_program(g, core, T, topo):
 
         for b in range(4):
             mm(4 + b, K, "qw", "sw", 128 * b, "qd", "sd", 0)
-        both("ca", 0, V("rw", 16, 16 + K), 16, 4)
+        both("ca", 0, V("rw", LO, LO + K), 16, 4)
         for b in range(4):
             if b % 2:
                 ts(V("h", b, 4 * K, 4), P(4 + b, K), 0.0, A.max, 0.015625, A.mult)
@@ -509,7 +537,8 @@ def rank_program(g, core, T, topo):
         ts(V("ou"), ind(V("tu"), V("lj", 12, 14)), 240.0, A.add)
         z_part("z2", 3, PL, cp)
         if r == ROUNDS - 1:
-            lin(V("plb"), V("c2", 16, 16 + K), 1.0, 160.0)
+            ts(V("rev"), V("small", 132, 142), QQ, A.subtract)
+            lin(V("plb"), ind(V("c2", 16, 16 + K), V("rev")), 1.0, 160.0)
             dma("y", T.pl[:], T.plb[KC:128:16, :], V("plb")[1], [], must=True)
         if r == 0:
             quant("qv", "sv", V("vin"))
@@ -533,7 +562,7 @@ def rank_program(g, core, T, topo):
     dma("y", T.y[:, 0:K], T.yb[:, 0:K], V("yb", 0, K)[1], [], must=True)
     for k in range(4):
         dma("s" if k < 2 else "y", T.osc[4 * k:4 * k + 4, :], T.sx[32 * k:32 * k + 4, :], V("sx")[1], [], must=True)
-    act(V("yb", K, C), P(1, K))
+    cp(V("yb", K, C), P(1, K))
     dma("s", T.y[:, K:C], T.yb[:, K:C], V("yb", K, C)[1], [], must=True)
 
     emit(g, T, ops)

from concourse.bass import DstId, RemoteDMATransfer
from concourse.mybir import dt, AluOpType, ActivationFunctionType

C, K, ROUNDS = 320, 160, 3
STEP = [1, 2, 4]
BIG = 1024
LO = 352
CX = C + 32
X4, U8, U16, BF, F32, I32 = "float8_e4m3fn_x4", "uint8", "uint16", "bfloat16", "float32", "int32"
SIZES = {
    BF: {"xin": 4 * C, "uin": 512, "vin": 512, "e0": 520, "ct": 1536, "row0": 448, "msk": C, "keep": 704, "cmp": 3840,
         "dg": 2 * C, "rd": 2 * C, "rs": 1536, "em": C, "et": C, "na": CX, "nb": CX + 4, "pj": 384, "tb": 2 * CX, "rw": 832, "tp": 352,
         "cr": 192, "tc": 352, "ca": K, "cb": K, "c2": 192, "td": 352, "ur": 352, "tu": 672, "thr": K,
         "fw": 4 * 480, "z": 4 * K, "z2": 4 * K, "h": 4 * K, "xn": 4 * C},
    F32: {"cf": 16, "small": 144, "ini": 160, "tab": 160, "ts": 2 * C, "acc": 8, "ce": 32, "cd": 32, "cst": 48,
          "l1": 80, "l2": 128, "l3": 80, "plb": K, "yb": C},
    I32: {"ci": 8, "lui": 16},
    U16: {"lu": 16, "lj": 16, "lc": 4, "le": 4, "osc1": 32, "ob": 32, "orr": 64, "rev": 10, "ocl": 16, "ou": 32},
    X4: {"qx": C, "qu": 128, "qu2": 256, "qv": 128, "qw": 512, "cq": 896, "cmq": 1216, "qa": K, "qb": K, "qc": K, "qd": K},
    U8: {"sx": C, "su": 128, "su2": 256, "sv": 128, "sw": 512, "cs": 896, "cms": 1216, "sa": K, "sb": K, "sc": K, "sd": K},
}
SCRATCH = {n: ("sbuf", [128, w], d) for d in SIZES for n, w in SIZES[d].items()}
for _r in range(ROUNDS):
    for _n in ("out", "hop", "land"):
        SCRATCH["%sq%d" % (_n, _r)] = ("sbuf", [128, K], X4)
        SCRATCH["%ss%d" % (_n, _r)] = ("sbuf", [128, K], U8)
for _b in range(8):
    SCRATCH["ps%d" % _b] = ("psum", [128, 512], F32)

POOL = {"v": 26, "s": 24, "t": 14, "g": 62, "d": 16}
SEMAPHORES = ["%s_%d" % (q, i) for q in POOL for i in range(POOL[q])]
SEMAPHORES += ["hop%d" % r for r in range(ROUNDS)] + ["arr%d" % r for r in range(ROUNDS)] + ["sent"]

A = AluOpType
ACT = ActivationFunctionType
KT, KC, KRP, KD, KRN, KZ, KF1, KF2, KF3 = range(9)
ADDED = ((KT, 0, 0, 1), (KD, 0, 0, -1), (KF1, 0, 0, -BIG), (KF2, 1, -1, BIG), (KF2, 1, 0, -BIG), (KF3, 1, 0, BIG), (KF3, 1, 1, -BIG))
SUMMED = ((KT, 1, 1, 1), (KRN, 1, 1, 1), (KRN, 1, 0, -1), (KRP, 1, 0, 1), (KRP, 1, -1, -1), (KD, 1, -1, -1))
START = {KT: -K, KC: -K, KF1: BIG, KF2: BIG, KF3: BIG, KD: K + 1}
TILE = [896, 768, 576, 320, 0]
ORDER = ("t00 t01 c10 t10 s90 c20 c11 c21 t11 s91 s80 s81 s70 s71 d00 d11 d01 d10 c30 c31 c40 c41 c50 q0 c51 m0 m1 c60 c61 f "
         "r90 r91 r80 r81 r70 r71 r61 k0 q4 k1 n2 n0 g n1 n3 q3 e q2")
LAST = "q2"
UPDATE = (("s", 0, 0), ("s", 1, 0), ("v", 2, 0), ("v", 3, 0), ("s", 0, 1), ("s", 1, 1), ("v", 3, 1), ("v", 4, 0), ("s", 2, 1), ("v", 4, 1))


def popcount(m):
    return bin(m).count("1")


def pieces_of(src, dst, topo):
    c = [k for k in topo.cores_of(src) if k != src and topo.may_write(k, dst)]
    near = [k for k in c if topo.die(k) == topo.die(src)]
    far = [k for k in c if topo.die(k) != topo.die(src)]
    e = topo.engines(src, near[0])
    half = len(e) // 2
    lo, hi = sum(1 << k for k in e[:half]), sum(1 << k for k in e[half:])
    return [(near[0], "q", 0, K // 2, lo, 0), (far[0], "q", K // 2, K, hi, 0), (near[1], "s", 0, K, lo | hi, 1)]


def side(T, name, r, piece):
    v = T["%s%s%d" % (name, piece[1], r)][:, piece[2]:piece[3]]
    return v.bitcast(dt.uint8) if piece[1] == "q" else v


def relay_program(g, core, T, topo):
    sent = 0
    for r in range(ROUNDS):
        for i, src in enumerate(T.cores):
            if core not in topo.cores_of(src):
                continue
            dst = T.cores[i ^ STEP[r]]
            mine = [p for p in pieces_of(src, dst, topo) if p[0] == core]
            if not mine:
                continue
            g.wait_ge(T.sem["hop%d" % r], sum(popcount(p[4]) for p in mine))
            rid, pid = topo.addr(dst, core)
            for p in mine:
                m = topo.mask(core, dst)
                g.remote_dma(side(T, "land", r, p), side(T, "hop", r, p), T.sem["arr%d" % r], T.sem.sent, pid, rid, m)
                sent += popcount(m)
    if sent:
        g.wait_ge(T.sem.sent, sent)


def overlap(a, b):
    if a[0] != b[0] or a[2] <= b[1] or b[2] <= a[1] or a[5] <= b[4] or b[5] <= a[4]:
        return False
    step = min(a[3], b[3])
    return not (step > 1 and max(a[3], b[3]) % step == 0 and a[1] % step != b[1] % step)


def emit(g, T, ops):
    Q = {"v": g.vector, "s": g.scalar, "t": g.tensor, "y": g.sync, "g": g}
    members = {}
    for i, o in enumerate(ops):
        members.setdefault(o["joint"] or i, []).append(i)
    rep = [members[o["joint"] or i][-1] for i, o in enumerate(ops)]
    known = {q: 0 for q in Q}
    at = [0] * len(ops)
    waits = [[] for _ in ops]
    seen = {}
    for i, o in enumerate(ops):
        deps = set()
        for kind in "rw":
            for reg in o[kind]:
                for (j, kj, rj) in seen.get(reg[0], []):
                    if rep[j] == rep[i]:
                        continue
                    if reg[0].startswith("ps") and ops[j]["q"] != o["q"]:
                        deps.add(rep[j])
                    elif (kind == "w" or kj == "w") and overlap(reg, rj):
                        deps.add(rep[j])
        for kind in "rw":
            for reg in o[kind]:
                seen.setdefault(reg[0], []).append((i, kind, reg))
        q = o["q"]
        for d in sorted(deps, reverse=True):
            assert d < i
            if not known[q] >> d & 1:
                waits[i].append(d)
                known[q] |= at[d] | 1 << d
        at[i] = known[q]
    signalled = set(d for w in waits for d in w) | set(rep[i] for i, o in enumerate(ops) if o["must"])
    pools = {k: [] for k in POOL}
    slot, value = {}, {}
    for i, o in enumerate(ops):
        q = o["q"]
        for d in waits[i]:
            Q[q].wait_ge(T.sem[slot[d][0]], value[d])
            slot[d][3] = max(slot[d][3], value[d])
        for (sem, val) in o["ext"]:
            Q[q].wait_ge(sem, val)
        ins = o["fn"]()
        if rep[i] in signalled:
            if rep[i] not in slot:
                kind = "d" if o["dma"] else q
                free = [] if o["dma"] else [s for s in pools[kind] if at[i] >> s[2] & 1]
                if free:
                    s = free[0]
                else:
                    s = ["%s_%d" % (kind, len(pools[kind])), 0, 0, 0]
                    pools[kind].append(s)
                s[2] = rep[i]
                slot[rep[i]] = s
            s = slot[rep[i]]
            inc = 16 if o["dma"] else 1
            ins.then_inc(T.sem[s[0]], inc)
            s[1] += inc
            value[rep[i]] = s[1]
    for k in pools:
        for s in pools[k]:
            if s[1] > s[3]:
                g.wait_ge(T.sem[s[0]], s[1])


def rank_program(g, core, T, topo):
    rank = T.rank_of(core)
    if rank is None:
        relay_program(g, core, T, topo)
        return
    ops = []

    def V(name, lo=0, hi=None, step=1, quad=None, tall=1):
        hi = T[name].shape[1] if hi is None else hi
        p0, p1 = (0, 128) if quad is None else (32 * quad, 32 * (quad + tall))
        cols = slice(lo, hi) if step == 1 else slice(lo, hi, step)
        ap = T[name][:, cols] if quad is None else T[name][p0:p1, cols]
        return (ap, [(name, lo, hi, step, p0, p1)])

    def ind(win, off):
        return (win[0].indirect(off[0]), win[1] + off[1])

    def val(s):
        return s[0] if isinstance(s, tuple) else s

    def regs(*xs):
        return [r for x in xs if isinstance(x, tuple) for r in x[1]]

    def op(q, fn, r, w, joint=None, dma=False, must=False, ext=()):
        ops.append({"q": q, "fn": fn, "r": r, "w": w, "joint": joint, "dma": dma, "must": must, "ext": ext})

    def ts(out, in0, s1, o0, s2=None, o1=None):
        if o1 is None:
            op("v", lambda: g.vector.tensor_scalar(out[0], in0[0], val(s1), None, o0), regs(in0, s1), out[1])
        else:
            op("v", lambda: g.vector.tensor_scalar(out[0], in0[0], val(s1), val(s2), o0, o1), regs(in0, s1, s2), out[1])

    def tt(out, a, b, o):
        op("v", lambda: g.vector.tensor_tensor(out[0], a[0], b[0], o), regs(a, b), out[1])

    def cp(out, a):
        op("v", lambda: g.vector.tensor_copy(out[0], a[0]), regs(a), out[1])

    def scatter(win, off, a):
        op("v", lambda: g.vector.tensor_copy(win[0].indirect(off[0]), a[0]), regs(a, off), win[1])

    def ms(out, c):
        op("v", lambda: g.vector.memset(out[0], c), [], out[1])

    def tr(out, a):
        op("v", lambda: g.vector.transpose(out[0], a[0]), a[1], out[1])

    def tr2(out, row, n, r0=16):
        tr(V(out, 0, n), V(row, r0, r0 + n))
        tr(V(out, n, 2 * n + 32), V(row, r0 - 16, r0 + n + 16))

    def scan(out, d0, d1, init, o0, o1):
        op("v", lambda: g.vector.tensor_tensor_scan(out[0], d0[0], d1[0], val(init), o0, o1), regs(d0, d1, init), out[1])

    def quant(q, s, a, c0=0, n=None):
        q, s = V(q, c0, None if n is None else c0 + n), V(s, c0, None if n is None else c0 + n)
        op("v", lambda: g.vector.quantize_mx(q[0], s[0], a[0]), regs(a), q[1] + s[1])

    def act(out, a, f=ACT.Copy, bias=None, scale=None, acc=None):
        kw = {}
        if bias is not None:
            kw["bias"] = val(bias)
        if scale is not None:
            kw["scale"] = val(scale)
        if acc is not None:
            kw["accum_out"] = acc[0]
        op("s", lambda: g.scalar.activation(out[0], a[0], f, **kw), regs(a, bias, scale), regs(out, acc))

    def lin(out, a, scale, bias):
        act(out, a, ACT.Identity, bias=bias, scale=scale)

    def pick(dst, src, off):
        q2, q1, s2, s1 = V("q" + dst), V("q" + src), V("s" + dst), V("s" + src)
        op("v", lambda: g.vector.tensor_copy(q2[0].bitcast(dt.uint32), q1[0].bitcast(dt.uint32).indirect(off[0])), regs(q1, off), q2[1])
        act(s2, ind(s1, off))

    def mm(bank, n, lq, ls, l0, rq, rs, r0, start=True, stop=True, joint=None, ext=()):
        o, a, b, c, d = V("ps%d" % bank, 0, n), V(lq, l0, l0 + 128), V(ls, l0, l0 + 128), V(rq, r0, r0 + n), V(rs, r0, r0 + n)
        op("t", lambda: g.tensor.matmul_mx(o[0], a[0], b[0], c[0], d[0], start, stop), regs(a, b, c, d), o[1], joint=joint, ext=ext)

    def iota(out, pat, base, cm=0, whole=False):
        if whole:
            op("g", lambda: g.iota(out[0], pat, base, cm), [], out[1])
        else:
            op("g", lambda: g.iota(out[0], pat, base, cm, allow_small_or_imprecise_dtypes=True), [], out[1])

    def fill(name, lo, hi, c, step=1):
        iota(V(name, lo, hi, step), [[0, len(range(lo, hi, step))]], c)

    def mark(out, pat, base, c):
        op("g", lambda: g.affine_select(out[0], out[0], pat, A.not_equal, c, base, 1), out[1], out[1])

    def dma(q, out, a, r, w, must=False):
        e = g.sync if q == "y" else g.scalar
        op(q, lambda: e.dma_start(out, a), r, w, dma=True, must=must)

    def P(b, n=C):
        return V("ps%d" % b, 0, n)

    def cf(k):
        return V("cf", k, k + 1)

    def ci(k):
        return V("ci", k, k + 1)

    dma("s", T.uin[:], T.u[:], [], V("uin")[1])
    for lo in (0, 2 * C):
        dma("y", T.xin[:, lo:lo + 2 * C], T.x[:, lo:lo + 2 * C], [], V("xin", lo, lo + 2 * C)[1])
    dma("y", T.qw[:].bitcast(dt.uint8), T.wc[:], V("xin")[1], V("qw")[1])
    dma("y", T.sw[:], T.ws[:], [], V("sw")[1])
    dma("y", T.vin[:], T.v[:], [], V("vin")[1])

    QUAD, CC, QQ, ODD, BIT, PAR, Q16, C304, CB, C336, C176, CR = [cf(k) for k in range(1, 13)]
    INIT, NA = V("tab", 0, 1), V("tab", 32, 33)
    ms(V("em"), 0.0)
    ms(V("e0"), 0.0)
    ms(V("ini"), 0.0)
    iota(ci(0), [[0, 1]], 0, 1, whole=True)
    iota(V("lui"), [[16, 2], [32, 4], [0, 2]], 0, whole=True)
    mark(V("e0", 4, 516, 4), [[-1, 128]], 0, 1.0)
    iota(V("row0", 0, 128), [[1, 4], [8, 2], [0, 16]], 0)
    iota(V("row0", 128, 128 + C), [[0, 10], [1, 32]], 0)
    for k in range(4):
        lin(V("ct", 512 + 256 * k, 768 + 256 * k), V("em", 0, 256), 0.0, 0.0)
    for k in range(2):
        lin(V("keep", 192 * k, 192 * (k + 1)), V("em", 0, 192), 0.0, 1.0)
    iota(V("small", 0, 32), [[-32, 16], [0, 2]], K - 31)
    for k in range(5):
        fill("cmp", 4 * (TILE[k] + 64 * k + 32) + (k < 4), 4 * (TILE[k] + 64 * k + 64), 0, 2)
    ts(ci(1), ci(0), 5, A.arith_shift_right)
    ts(ci(2), ci(0), 31, A.bitwise_and)
    ts(ci(3), ci(0), 15, A.bitwise_and)
    ts(ci(4), ci(0), 4, A.arith_shift_right, 1, A.bitwise_and)
    ts(ci(5), ci(0), 1, A.bitwise_and)
    cp(V("lu"), V("lui"))
    cp(V("cf", 1, 6), V("ci", 1, 6))
    for b in range(4):
        quant("cq", "cs", V("e0", 4 - b, 516 - b), 128 * b, 128)
    for t in range(4):
        ts(V("ct", t, 512, 4), V("row0", 0, 128), -8.0 * (t // 2), A.add, QUAD, A.is_equal)
    quant("qu", "su", V("uin"))
    quant("cmq", "cms", V("ct", 512, 1024), 960, 128)
    op("v", lambda: g.vector.tensor_copy(T.qu2[:, 0:256].bitcast(dt.uint32), T.qu[:, 0:128].bitcast(dt.uint32).indirect(T.lu[:, 0:16])),
       regs(V("qu"), V("lu")), V("qu2")[1])
    act(V("su2"), ind(V("su"), V("lu")))
    for lo in (0, K):
        quant("qx", "sx", V("xin", 4 * lo, 4 * (lo + K)), lo, K)
    quant("cmq", "cms", V("ct", 1024, 1536), 1088, 128)
    quant("cq", "cs", V("ct", 0, 512), 512, 128)
    ts(V("msk"), V("row0", 128, 128 + C), CC, A.is_lt, -1.0, A.mult)
    act(V("keep", 384, 384 + C), V("row0", 128, 128 + C), ACT.Sign)
    lin(V("rs", 1152, 1344), V("em", 0, 192), 0.0, 0.0)
    lin(V("ce"), V("small", 0, 32), 1.0, CC)
    act(PAR, BIT, ACT.Abs, bias=ODD, scale=-1.0)
    lin(Q16, QQ, 16.0, 0.0)
    lin(C304, BIT, 304.0, Q16)
    lin(CB, PAR, 16.0 - CX, Q16)
    lin(C336, PAR, 336.0, Q16)
    lin(C176, PAR, 176.0, Q16)
    lin(CR, ODD, -16.0, C176)

    fill("keep", 192, 384, 0, 128)
    iota(V("small", 128, 130), [[256, 2]], 31)
    fill("ini", 64, 80, 1152)
    for k in range(3):
        iota(V("ini", 66 + 4 * k, 70 + 4 * k), [[384, 2], [768, 2]], 383 - 32 * k * (k + 1))
    for k in START:
        fill("ini", k, 32, START[k], 16)
    fill("ini", KRP, KRP + 1, BIG)
    fill("ini", 32 + KC, 64, 1, 16)
    fill("ini", 32 + KD, 33 + KD, -1)
    for base, table in ((512, ADDED), (1024, SUMMED)):
        for kind, odd, line, w in table:
            step = 16 << odd
            mark(V("ct", base + 4 * (16 * odd + kind) + 1, base + 512, 4 * step), [[-step, 128 // step]], -16 * (odd + line), float(w))
    fill("pj", 0, 16, 0)
    for odd, first, turn in ((0, CX, 32 - CX), (1, 16, CX)):
        iota(V("ini", 96 + 16 * odd, 112 + 16 * odd), [[32, 2], [turn, 2], [1, 4]], first + KZ)
        iota(V("ini", 128 + 16 * odd, 144 + 16 * odd), [[32, 4], [turn, 2], [1, 2]], first + KD)
    iota(V("small", 32, 38), [[64, 6]], 0)
    iota(V("small", 38, 42), [[128, 4]], 0)
    iota(V("small", 42, 44), [[256, 2]], CX + KRP)
    iota(V("small", 44, 46), [[256, 2]], 0)
    iota(V("small", 48, 80), [[16, 32]], K + 1)
    iota(V("cst"), [[0, 24], [K + 2 - LO, 2]], 0)
    iota(V("small", 46, 48), [[KT - KC, 2]], KC)
    iota(V("small", 80, 128), [[0, 3], [16, 16]], 0)
    iota(V("rw", 0, K + 1), [[1, K + 1]], -K - 1)
    fill("rw", K + 1, LO, 0)
    fill("rw", LO + K, LO + K + 16, 0)
    for name, n in (("cr", K), ("c2", K), ("ur", C)):
        fill(name, 0, 16, 0)
        fill(name, 16 + n, T[name].shape[1], 0)
    iota(V("thr"), [[1, K]], 80)
    iota(V("small", 132, 142), [[-16, 10]], K - 1)

    sent = 0
    for r in range(ROUNDS):
        partner = T.cores[rank ^ STEP[r]]
        iota(V("ur", 16, 16 + C), [[1, C]], -240)
        for bank, hh, lo, n in ((6, 0, 0, K), (7, 1, 0, K), (4, 0, K, K), (2, 0, 0, 288), (0, 1, K, K), (3, 1, 0, 288), (1, 0, 0, 192), (5, 1, 0, 192)):
            mm(bank, n, "qu2", "su2", 128 * hh, "qx", "sx", lo)

        def slot(b, hh):
            c0 = 4 * TILE[(b - 1) // 2]
            return V("cmp", c0 + 2 * hh + (b % 2 if b < 9 else 0), c0 + 128 * b, 4)

        def sums(k, n, first=False, last=False):
            mm(0, n, "cq", "cs", 512, "cmq", "cms", TILE[k], start=first, stop=last, joint="rank%d" % r)

        for step in ORDER.split():
            kind = step[0]
            b, hh = int((step + "00")[1]), int((step + "00")[2])
            s = V("ts", C * hh + 32 * b, C * hh + 32 * b + 1)
            if kind == "c":
                ts(slot(b, hh), P(1 + 4 * hh if b == 6 else 6 + hh, 32 * b), s, A.is_lt)
            elif kind == "s":
                act(slot(b, hh), P(2 + hh, 32 * b), ACT.Sign, bias=s, scale=-1.0)
            elif kind == "r":
                e = 2 * b + hh - 13
                act(slot(b, hh), slot(b, hh), ACT.Relu, acc=V("acc", e, e + 1))
            elif kind in "td":
                bank, o = P((6, 7, 4, 0)[2 * b + hh], K), C * hh + K * b
                if kind == "t":
                    tr(V("ts", o, o + K), bank)
                else:
                    tt(V("dg", o, o + K), bank, V("ts", o, o + K), A.is_ge)
            elif kind == "m":
                scan(V("cmp", 2 * b + 1, 4 * C, 4), V("dg", C * b, C * (b + 1)), V("msk"), 0.0, A.max, A.mult)
            elif kind == "k":
                scan(V("rd", C * b, C * (b + 1)), V("keep", 384, 384 + C), V("cmp", 2 * b + 1, 4 * C, 4), 0.0, A.mult, A.add)
            elif kind == "n":
                lo = 192 if b == 2 else 0
                o = 384 * (1, 0, 3, 2)[b]
                scan(V("rs", o + lo, o + 384), V("keep", lo, 384), V("cmp", 4 * (TILE[2] + lo) + b, 3840, 4), 0.0, A.mult, A.add)
            elif kind == "q":
                n = 192 if b == 0 else 64 * (b + 1)
                c0 = TILE[max(b, 1)]
                quant("cmq", "cms", V("cmp", 4 * c0, 4 * (c0 + n)), c0, n)
                if b == 0:
                    sums(0, C, first=True)
                    sums(1, 128)
                else:
                    sums(b, n, last=step == LAST)
            elif kind == "f":
                for b in range(4):
                    mm(4 + b, C, "cq", "cs", 128 * b, "qx", "sx", 0)
            elif kind == "g":
                tt(V("cd"), ind(V("rd"), V("le", 2, 4)), V("ce"), A.add)
            else:
                tt(V("em", 0, 256, 16), ind(V("rs"), V("le", 0, 1)), V("cd", 0, 16), A.add)
            if r == 0 and step == "q0":
                cp(V("ini", 80, 96), V("ini", 64, 80))
            if r == 0 and step == "k0":
                tr(V("tab", 0, 96), V("ini", 0, 96))
                ts(V("le", 2, 4), V("small", 128, 130), C304, A.add, 2.0 * C - 1, A.min)
            if r == 0 and step == "k1":
                cp(V("le", 0, 1), V("tab", 64, 65))

        def f_out(b):
            act(V("fw", 480 * b, 480 * b + C), P(4 + b))

        tt(V("em", 208, C, 16), V("acc", 0, 7), V("cd", 13, 20), A.add)
        tr(V("et"), V("em"))
        if r == 0:
            quant("cq", "cs", V("ct", 1024, 1536), 768, 128)
            lin(V("na", 0, CX), V("e0", 0, CX), 0.0, NA)
            lin(V("nb", 0, 1), INIT, 1.0, 0.0)
        HALVES = ((0, K, 2, 1), (K, CX, 3, 0))
        for lo in (0, K):
            tt(V("cmp", 4 * lo + 1, 4 * (lo + K), 4), V("ps0", lo, lo + K), V("et", lo, lo + K), A.is_lt)
        for lo, hi, b2, b1 in HALVES:
            quant("cmq", "cms", V("cmp", 4 * lo, 4 * (lo + K)), 640 + lo, K)
            mm(b2, hi - lo, "cq", "cs", 768, "cmq", "cms", 640 + lo)
            if r == 0 and lo == 0:
                quant("cq", "cs", V("ct", 512, 1024), 640, 128)
            mm(b1, hi - lo, "cq", "cs", 640, "cmq", "cms", 640 + lo)
        for b in range(4):
            f_out(b)
        if r == 0:
            lin(V("l2", 0, 128, 4), V("small", 48, 80), 1.0, QQ)
            tr(V("tab", 96, 160), V("ini", 96, 160))
            ts(V("lj", 10, 12), V("small", 42, 44), CB, A.add, CX + C - 1.0, A.min)

        for lo, hi, b2, b1 in HALVES:
            scan(V("nb", 1 + lo, 1 + hi), P(b2, hi - lo), V("na", lo, hi), V("nb", lo, lo + 1), A.add, A.add)
            if lo:
                tr(V("tb", 0, K), V("pj", 0, K))
            elif r == 0:
                ts(V("lj", 0, 6), V("small", 32, 38), V("tab", 96, 97), A.add, CX + C - 1.0, A.min)
            scan(V("pj", 16 + lo, 16 + hi), V("nb", lo, hi), P(b1, hi - lo), V("pj", 15 + lo, 16 + lo) if lo else INIT, A.max, A.add)
        tr(V("tb", CX, CX + K), V("pj", 16, 16 + K))
        if r == 0:
            ts(V("lj", 6, 10), V("small", 38, 42), V("tab", 128, 129), A.add, CX + C - 1.0, A.min)
        tr(V("tb", CX + K, 2 * CX), V("pj", 16 + K, 16 + CX))
        tr(V("tb", K, CX), V("pj", K, CX))

        def got(lo, hi):
            return ind(V("tb", 0, CX + C), V("lj", lo, hi))

        lin(V("l2", 2, 128, 4), got(10, 12), -1.0, V("tb", CX + C + 16 + KRP, CX + C + 17 + KRP))
        tt(V("l2", 1, 96, 2), got(6, 9), V("cst"), A.add)
        lin(V("l1", 0, 32), got(0, 2), 1.0, -400.0)
        ts(V("l1", 32, 80), got(2, 5), -400.0, A.add)
        if r == 0:
            ts(V("lc", 0, 2), V("small", 46, 48), C176, A.add, 351.0, A.min)
        scan(V("l3"), V("l1"), V("l2", 0, 80), 0.0, A.min, A.max)
        if r == 0:
            ts(V("lc", 2, 3), CR, 16.0 + KT, A.add, 351.0, A.min)
        ts(V("osc1", 0, 20), V("l3", 3, 80, 4), LO - 1.0, A.add)
        if r == 0:
            ts(V("orr", 16, 64), V("small", 80, 128), QQ, A.add)
        scatter(V("rw"), V("osc1", 0, 20), V("pj", 16, 16 + C))
        tr2("tp", "rw", K, LO)
        if r == 0:
            ts(V("lj", 12, 14), V("small", 44, 46), C336, A.add, 671.0, A.min)
        ts(V("ob"), ind(V("tp"), V("lc", 0, 2)), 160.0, A.add)

        def z_part(name, b, lst, e):
            e(V(name, b, 4 * K, 4), ind(V("fw", 480 * b, 480 * b + C), lst))

        def hand(stage, src, up, tall=1):
            cp(V("orr", 16 * stage, 16 * stage + 10, quad=src + up, tall=tall), V("orr", 0, 10, quad=src, tall=tall))

        L1 = V("ob", 0, 10)
        act(V("cr", 16, 16 + K), ind(V("rw", 0, LO - 16), V("ob", 16, 26)))
        z_part("z", 0, L1, cp)
        z_part("z", 2, L1, act)
        z_part("z", 1, L1, cp)
        tr2("tc", "cr", K)
        z_part("z", 3, L1, act)
        ts(V("orr", 0, 16), ind(V("tc"), V("lc", 2, 3)), -1.0, A.mult, -1.0, A.add)
        quant("qa", "sa", V("z"))
        hand(1, 2, 1)
        hand(1, 1, 1)
        hand(2, 0, 2, 2)
        pick("b", "a", V("orr", 16, 26))
        hand(3, 0, 3)
        hand(3, 0, 1)
        pick("c", "b", V("orr", 32, 42))
        pick("d", "c", V("orr", 48, 58))

        def both(dst, d0, src, lst, n):
            act(V(dst, d0, d0 + 16 * n), ind(src, V("orr", lst, lst + n)))
            cp(V(dst, d0 + 16 * n, d0 + K), ind(src, V("orr", lst + n, lst + 10)))

        for b in range(4):
            mm(4 + b, K, "qw", "sw", 128 * b, "qd", "sd", 0)
        both("ca", 0, V("rw", LO, LO + K), 16, 4)
        for b in range(4):
            if b % 2:
                ts(V("h", b, 4 * K, 4), P(4 + b, K), 0.0, A.max, 0.015625, A.mult)
            else:
                act(V("h", b, 4 * K, 4), P(4 + b, K), ACT.Relu, scale=0.015625)
        quant("outq%d" % r, "outs%d" % r, V("h"))

        pieces = pieces_of(core, partner, topo)

        def send(r=r, pieces=pieces):
            for call in sorted(set(p[5] for p in pieces)):
                tx = []
                for p in pieces:
                    if p[5] == call:
                        rid, pid = topo.addr(p[0], core)
                        tx.append(RemoteDMATransfer(dst_ids=[DstId(rid=rid, pnc=pid)], dma_engine_mask=p[4], remote_sem=T.sem["hop%d" % r],
                                                    src=side(T, "out", r, p), dst=side(T, "hop", r, p)))
                g.remote_dma_fused(tx, local_sem=T.sem.sent)

        op("g", send, regs(V("outq%d" % r), V("outs%d" % r)), [])
        sent += sum(popcount(p[4]) for p in pieces)

        both("cb", 0, V("ca"), 32, 4)
        both("c2", 16, V("cb"), 48, 4)
        tr2("td", "c2", K)
        ts(V("ocl"), ind(V("td"), V("lc", 0, 1)), 160.0, A.add)
        PL = V("ocl", 0, 10)
        for b in range(3):
            z_part("z2", b, PL, act)
        scatter(V("ur", 16, 16 + C), PL, V("thr"))
        tr2("tu", "ur", C)
        ts(V("ou"), ind(V("tu"), V("lj", 12, 14)), 240.0, A.add)
        z_part("z2", 3, PL, cp)
        if r == ROUNDS - 1:
            ts(V("rev"), V("small", 132, 142), QQ, A.subtract)
            lin(V("plb"), ind(V("c2", 16, 16 + K), V("rev")), 1.0, 160.0)
            dma("y", T.pl[:], T.plb[KC:128:16, :], V("plb")[1], [], must=True)
        if r == 0:
            quant("qv", "sv", V("vin"))

        arrive = sum(popcount(topo.mask(p[0], core)) for p in pieces_of(partner, core, topo))
        for b in range(4):
            mm(4 + b, K, "cq", "cs", 128 * b, "landq%d" % r, "lands%d" % r, 0, ext=[(T.sem["arr%d" % r], arrive)] if b == 0 else ())
        for b in range(4):
            tt(V("fw", 480 * b + C, 480 * b + 480), P(4 + b, K), V("z2", b, 4 * K, 4), A.add)
        for e, b, hf in UPDATE:
            if b < 4:
                (cp if e == "v" else act)(V("xn", 2 * C * hf + b, 2 * C * (hf + 1), 4), ind(V("fw", 480 * b, 480 * b + 480), V("ou", 10 * hf, 10 * hf + 10)))
            else:
                quant("qx", "sx", V("xn", 2 * C * hf, 2 * C * (hf + 1)), K * hf, K)

    mm(0, K, "qv", "sv", 0, "qx", "sx", 0)
    mm(1, K, "qv", "sv", 0, "qx", "sx", K)
    for lo in (0, K):
        dma("y", T.oc[:, 4 * lo:4 * (lo + K)], T.qx[:, lo:lo + K].bitcast(dt.uint8), V("qx", lo, lo + K)[1], [], must=True)
    cp(V("yb", 0, K), P(0, K))
    dma("y", T.y[:, 0:K], T.yb[:, 0:K], V("yb", 0, K)[1], [], must=True)
    for k in range(4):
        dma("s" if k < 2 else "y", T.osc[4 * k:4 * k + 4, :], T.sx[32 * k:32 * k + 4, :], V("sx")[1], [], must=True)
    cp(V("yb", K, C), P(1, K))
    dma("s", T.y[:, K:C], T.yb[:, K:C], V("yb", K, C)[1], [], must=True)

    emit(g, T, ops)
    g.wait_ge(T.sem.sent, sent)
